import numpy as np, ml_dtypes
CORES = [48,51,52,55]
N = 4
BF = ml_dtypes.bfloat16
def gentries(a):
    return np.ascontiguousarray(a.reshape(8, 16, -1).transpose(0, 2, 1)).reshape(8, -1)
def gtable(e):
    e = np.asarray(e); return np.ascontiguousarray(e.reshape(8, -1, 16).transpose(0, 2, 1)).reshape(128, -1).astype(np.int32)
W, L, M, B, TS, CAP = 8192, 256, 4, 4, 4, 128
R = M * B
KAPPA = (3, 29, 71, 113)
def run(x, z, v):
    tr = []
    for b in range(B):
        u = np.add.reduce(z, axis=2)
        c = np.concatenate([((u * u >> 4) + k * u + v) & (W - 1) for k in KAPPA], axis=2)
        y = np.take_along_axis(x, c[:, :, None, :], 3).reshape(N, 8, 16, M, L)
        z = np.abs(np.maximum.reduce(y, axis=3) - z)
        tr.append(c)
    return z, np.concatenate(tr, axis=2)
def starts(z, h, fr):
    halt = (~fr) & (np.add.reduce((z >= h[..., None]).astype(np.int64), axis=2) >= 9)
    slot = np.add.accumulate(halt.astype(np.int64), axis=2) - halt
    return halt & (slot < CAP)
def parts(rng):
    return rng.integers(0, 256, (N, 8, 16, W)), rng.integers(0, 256, (N, 8, 16, L)), rng.integers(0, W, (N, 8, L))
def levels(rng, x, s, v, share):
    j = rng.integers(-24, 25, (N, 8, 16, TS)); z = run(x, s, v)[0]; th = np.zeros((N, 8, 16, TS), np.int64)
    for t in range(TS):
        k = np.sort(np.sort(z - j[..., t:t + 1], axis=2)[:, :, 7], axis=2)
        n = np.minimum(np.maximum((share[..., t] * L).astype(np.int64), 1), L)
        th[..., t] = np.take_along_axis(k, (L - n)[..., None], 2) + j[..., t]
    return np.minimum(np.maximum(th, 0), 255)
def pack(x, s, v, th):
    return {"x": x.reshape(N, 128, W).astype(np.float32).astype(BF), "sd": s.reshape(N, 128, L).astype(np.float32).astype(BF),
            "v0": np.stack([gtable(a) for a in v]), "th": np.ascontiguousarray(th.reshape(N, 128, TS)).astype(np.int32)}
def shares(rng):
    return rng.choice(np.array([0.1, 0.25, 0.4, 0.6]), (N, 8, TS))
def setup_inputs(rng):
    x, s, v = parts(rng)
    return pack(x, s, v, levels(rng, x, s, v, shares(rng)))
def setup_inputs_claims(rng):
    x, s, v = parts(rng); share = rng.choice(np.array([0.2, 0.35, 0.45]), (N, 8, TS)); th = levels(rng, x, s, v, share)
    z, c = run(x, s, v); go = starts(z, th[..., 0], np.zeros((N, 8, L), bool))
    for r in range(0, N, 2):
        for g in range(8):
            j = np.nonzero(go[r + 1, g])[0]
            if len(j) == 0: j = np.arange(L)
            e = rng.choice(np.array([0, R - 1, -1]), L); e = np.where(e < 0, rng.integers(0, R, L), e)
            v[r, g] = np.where(rng.random(L) < 0.6, c[r + 1, g, e * L + rng.choice(j, L)], v[r, g])
    th[0::2] = levels(rng, x, s, v, share)[0::2]
    th[1, :, :, 1] = 255; th[:, 5, :, 2] = 255; th[2, :, :, TS - 1] = 255
    return pack(x, s, v, th)
def setup_inputs_corners(rng):
    x, s, v = parts(rng); v = np.ascontiguousarray(np.argsort(rng.random((N, 8, W)), axis=-1)[..., :L])
    pm = np.ones((N, 8), bool); pm[2:, 6:] = False
    x = np.where(pm[:, :, None, None], 255, x)
    n = rng.choice(np.array([0, 1, CAP - 1, CAP, CAP + 1, L]), (N, 8)); n[0] = 0
    n[1] = np.array([CAP, CAP + 1, L, CAP, L, CAP + 1, CAP, L]); n[2] = np.array([CAP, CAP + 1, L, CAP - 1, 1, 0, CAP, CAP])
    hot = np.argsort(np.argsort(rng.random((N, 8, L)), axis=2), axis=2) < n[:, :, None]
    k = np.where(hot, np.where(rng.random((N, 8, L)) < 0.5, 9, rng.integers(9, 17, (N, 8, L))), np.where(rng.random((N, 8, L)) < 0.5, 8, rng.integers(0, 9, (N, 8, L))))
    up = np.argsort(np.argsort(rng.random((N, 8, 16, L)), axis=2), axis=2) < k[:, :, None, :]
    tb = rng.integers(1, 256, (N, 8, 16)); tb[:, 1] = 1; tb[:, 3] = 255; tb[:, 5] = rng.choice(np.array([1, 255]), (N, 16))
    b = tb[..., None]; near = rng.random(s.shape) < 0.5
    hi = np.where(near, b, b + ((256 - b) * rng.random(s.shape)).astype(np.int64)); lo = np.where(near, b - 1, (b * rng.random(s.shape)).astype(np.int64))
    s = np.where(pm[:, :, None, None], np.where(up, hi, lo), s)
    th = levels(rng, x, s, v, shares(rng)); th[..., 0] = np.where(pm[:, :, None], tb, th[..., 0])
    return pack(x, s, v, th)
def setup_inputs_ends(rng):
    x, s, v = parts(rng); one = 1.0
    for i in range(M.bit_length() - 1): one = one * 0.5
    a = rng.random((N, 8, 1, W)); x = np.where(a < 0.4 * one, 255, np.where(a < 1.2 * one, 255 * rng.integers(0, 2, x.shape), 0))
    a = rng.random((N, 8, 1, L)); s = np.where(a < 0.35, 255, np.where(a < 0.6, 0, 255 * rng.integers(0, 2, s.shape)))
    v = np.where(rng.random(v.shape) < 0.72, (W - 1) * rng.integers(0, 2, v.shape), v)
    x[:, 1::2, :, W - 1] = 255; x[:, 0::2, :, W - 1] = 0; x[:, :, :, 0] = 255 - x[:, :, :, W - 1]
    s[:, 1::2, :, L - 1] = 255; s[:, 0::2, :, L - 1] = 0; s[:, :, :, 0] = 255 - s[:, :, :, L - 1]; s[:, 1::2, :, 5] = 255; s[:, 1::2, :, L - 4] = 255
    v[:, :, L - 1] = W - 1; v[:, :, L - 4] = W - 1; v[:, :, 5] = W - 1; v[:, :, 0] = 0
    k = rng.choice(np.array([16, 16, 12, 10, 9, 8, 8, 7, 0]), (N, 8, 1, TS)); k[:, 7, :, 0] = 12; k[:, 6, :, 0] = 0; k[:, 0, :, TS - 1] = 9; k[:, 7, :, TS - 1] = 16
    th = np.where(np.argsort(np.argsort(rng.random((N, 8, 16, TS)), axis=2), axis=2) < k, 255, 0)
    return pack(x, s, v, th)
def setup_inputs_spread(rng):
    x, s, v = parts(rng)
    x = np.minimum((np.exp2(1 + 7 * rng.random((N, 8, 1, W))) * rng.random(x.shape)).astype(np.int64), 255)
    s = np.minimum((np.exp2(1 + 7 * rng.random((N, 8, 1, L))) * rng.random(s.shape)).astype(np.int64), 255)
    v = np.minimum((W * rng.random(v.shape) ** 3).astype(np.int64), W - 1)
    return pack(x, s, v, levels(rng, x, s, v, shares(rng)))
def setup_inputs_ties(rng):
    x, s, v = parts(rng); pool = rng.integers(0, W, (8, 12)); pool[:, 0] = 0; pool[:, 1] = W - 1; h = L // 2; q = L // 4
    v = np.stack([pool[g][rng.integers(0, 12, (N, L))] for g in range(8)], axis=1)
    s[..., h:] = s[..., :h]; v[..., h:] = np.where(rng.random((N, 8, h)) < 0.5, v[..., :h], v[..., h:])
    pl = [2, 4, 7]; x[:, 2] = 255; x[:, 4] = 0; x[:, 7] = 0
    s[:, pl] = rng.integers(0, 100, (N, 3, 16, L))
    for a in range(0, N, 2):
        b = a + 1
        k = int(rng.integers(1, 4)); p = int(v[b, 2, 0])
        s[b, 2, :, k * q:(k + 1) * q] = 255; v[b, 2, k * q:(k + 1) * q] = p
        s[a, 2, :, (k - 1) * q:k * q] = rng.integers(201, 256, (16, q))
        v[a, 2, (k - 1) * q:k * q] = np.where(rng.random(q) < 0.8, p, v[a, 2, (k - 1) * q:k * q]); v[a, 2, (k - 1) * q] = p
        ln = np.append(q + rng.permutation(3 * q - 1)[:3], L - 1); e = rng.integers(201, 252, 4); pv = 16 * rng.permutation(W // 16)[:4] + 1; u = 16 * e
        s[b, 4][:, ln] = e; v[b, 4][ln] = pv
        wr = rng.permutation(q)[:4 * M]; s[a, 4][:, wr] = rng.integers(201, 252, 4 * M); s[a, 4][5, wr] += 4
        v[a, 4][wr] = np.concatenate([((u * u >> 4) + m * u + pv) & (W - 1) for m in KAPPA])
        p = W - 2 if a == 0 else int(rng.integers(W // 2, W - 1))
        for l, c in ((0, p + 1), (h, p)):
            s[b, 7, :, l] = rng.integers(201, 256, 16); u = int(np.sum(s[b, 7, :, l])); v[b, 7, l] = (c - (u * u >> 4) - KAPPA[0] * u) & (W - 1)
        for l, c in ((3, p + 1), (L - 1, p)):
            s[a, 7, :, l] = rng.integers(201, 256, 16); v[a, 7, l] = c
    th = levels(rng, x, s, v, shares(rng)); th[..., 0][:, pl] = rng.integers(100, 201, (N, 3, 16))
    return pack(x, s, v, th)
def check_inputs(d):
    bad = []
    for k, lo, hi in (("x", 0, 255), ("sd", 0, 255), ("v0", 0, W - 1), ("th", 0, 255)):
        a = np.asarray(d[k]).astype(np.float64)
        if not (np.min(a) >= lo and np.max(a) <= hi): bad.append("range of " + k)
        elif np.any(np.floor(a) != a): bad.append("whole numbers in " + k)
    return bad
def reference(x, sd, v0, th):
    X = x.astype(np.float32).astype(np.int64).reshape(N, 8, 16, W); S = sd.astype(np.float32).astype(np.int64).reshape(N, 8, 16, L)
    H = th.astype(np.int64).reshape(N, 8, 16, TS); v = np.stack([gentries(a) for a in v0]).astype(np.int64)
    fr = np.zeros((N, 8, L), bool); tr = np.zeros((N, 8, R * L), np.int64); cl = np.arange(L) * 4 // L
    for t in range(TS):
        z, c = run(X, S, v)
        tr = np.where(np.tile(fr, (1, 1, R)), tr, c)
        go = starts(z, H[..., t], fr); fr = fr | go
        back = np.zeros((N, 8, L), bool); hurt = np.zeros((N, 8, L), bool); done = np.zeros((N, 1, 1), np.int64)
        for q in range(N):
            p = q ^ (1 + t % (N - 1))
            for g in range(8):
                ln = np.nonzero(go[p, g])[0]; w = v[p, g, ln]
                mark = np.full(W, 9); np.minimum.at(mark, tr[q, g], np.where(np.tile(fr[q, g], R), np.tile(cl, R), 9))
                ok = np.nonzero(mark[w] > cl[ln])[0]
                win = np.zeros(len(ln), bool); win[ok[np.unique(w[ok], return_index=True)[1]]] = True
                back[p, g, ln[~win]] = True; done[q, 0, 0] += np.count_nonzero(win)
                if t < TS - 1: X[q, g][:, w[win]] = z[p, g][:, ln[win]]
                hit = np.zeros(W, bool); hit[w[win]] = True
                hurt[q, g] = fr[q, g] & np.any(hit[tr[q, g]].reshape(R, L), axis=0)
        fr = fr & (~back) & (~hurt)
        v = np.where(fr, v, (((v & 4095) ** 2 >> 3) + 37 * v + done) & (W - 1))
    ys = np.concatenate([v, fr.astype(np.int64)], axis=2)
    return {"yt": np.stack([gtable(a) for a in tr]).astype(np.float32), "ys": np.stack([gtable(a) for a in ys]).astype(np.float32)}

@@ -1,0 +1,568 @@
+from concourse.mybir import AluOpType as Op, AxisListType, ActivationFunctionType as AF
+
+W, L, D = 8192, 256, 8448
+KAPPA = (3, 29, 71, 113)
+TS, CAP = 4, 128
+FL = "GO THR OK L1 L2 LF IW LD E1 E2 FR FS VF VD BA S4 S5 S6".split()
+IL = "VN VC S1 S2 S3 S7".split()
+CM = "ID NI N5 BO TG ON".split()
+
+SCRATCH = {
+    "X": ("sbuf", [128, 8448], "bfloat16"),
+    "QA": ("sbuf", [128, 8464], "bfloat16"), "QB": ("sbuf", [128, 8464], "bfloat16"), "HT": ("sbuf", [128, 8464], "bfloat16"),
+    "IO": ("sbuf", [128, 8192], "float32"),
+    "SD": ("sbuf", [128, 256], "bfloat16"), "V0": ("sbuf", [128, 16], "int32"), "TI": ("sbuf", [128, 4], "int32"), "TF": ("sbuf", [128, 4], "float32"),
+    "PI": ("sbuf", [128, 4], "int32"), "PF": ("sbuf", [128, 4], "float32"),
+    "RM": ("sbuf", [128, 256], "float32"), "RD": ("sbuf", [128, 256], "float32"), "RP": ("sbuf", [128, 128], "float32"), "RG": ("sbuf", [128, 128], "float32"),
+    "K1": ("sbuf", [128, 256], "float32"), "K2": ("sbuf", [128, 256], "float32"), "K3": ("sbuf", [128, 256], "float32"), "K4": ("sbuf", [128, 256], "float32"),
+    "CM": ("sbuf", [128, 128 * len(CM)], "bfloat16"), "FL": ("sbuf", [128, 16 * len(FL)], "float32"), "IL": ("sbuf", [128, 16 * len(IL)], "int32"),
+    "NM": ("sbuf", [128, 256], "bfloat16"), "CO": ("sbuf", [128, 256], "bfloat16"), "D0": ("sbuf", [128, 256], "float32"),
+    "TH": ("sbuf", [128, 128], "float32"), "WH": ("sbuf", [128, 2], "float32"), "DM": ("sbuf", [128, 16], "float32"),
+    "OB": ("sbuf", [128, 256], "bfloat16"), "ZB": ("sbuf", [128, 264], "bfloat16"),
+    "TN": ("sbuf", [128, 256], "int32"), "TR": ("sbuf", [128, 256], "float32"), "P1": ("sbuf", [128, 256], "float32"),
+    "P2": ("sbuf", [128, 256], "float32"), "M1": ("sbuf", [128, 256], "float32"), "M2": ("sbuf", [128, 256], "float32"),
+    "OM": ("sbuf", [128, 256], "uint16"), "NG": ("sbuf", [128, 256], "bfloat16"), "NF": ("sbuf", [128, 256], "bfloat16"), "FO": ("sbuf", [128, 256], "bfloat16"),
+    "OV": ("sbuf", [128, 16], "uint16"), "DV": ("sbuf", [128, 256], "uint16"), "OD": ("sbuf", [128, 16], "uint16"),
+    "HA": ("sbuf", [128, 16], "bfloat16"), "SC": ("sbuf", [128, 18], "bfloat16"),
+    "EB": ("sbuf", [128, 16, 256], "bfloat16"), "DUL": ("sbuf", [128, 256], "float32"), "HUL": ("sbuf", [128, 256], "float32"),
+    "MC": ("sbuf", [128, 128], "bfloat16"), "MD": ("sbuf", [128, 64], "bfloat16"), "ME": ("sbuf", [128, 32], "bfloat16"), "MF": ("sbuf", [128, 16], "bfloat16"),
+    "AA": ("sbuf", [128, 1], "float32"), "YT": ("sbuf", [128, 16, 16], "float32"), "YS": ("sbuf", [128, 32], "float32"),
+    "GB": ("sbuf", [128, 4096], "bfloat16"), "HB": ("sbuf", [128, 2048], "bfloat16"), "LA": ("sbuf", [128, 2048], "bfloat16"), "LB": ("sbuf", [128, 2048], "bfloat16"),
+    "pU0": ("psum", [128, 512], "float32"), "pU1": ("psum", [128, 512], "float32"), "pD0": ("psum", [128, 512], "float32"), "pD1": ("psum", [128, 512], "float32"),
+    "pT0": ("psum", [128, 1024], "bfloat16"), "pT1": ("psum", [128, 1024], "bfloat16"), "pC": ("psum", [128, 512], "float32"), "pH": ("psum", [128, 512], "float32"),
+}
+for _h in range(2):
+    SCRATCH.update({"Z%d" % _h: ("sbuf", [128, 128], "bfloat16"), "Y%d" % _h: ("sbuf", [128, 128], "bfloat16"), "A%d" % _h: ("sbuf", [128, 128], "bfloat16"),
+                    "B%d" % _h: ("sbuf", [128, 128], "bfloat16"), "C%d" % _h: ("sbuf", [128, 128], "bfloat16"), "F%d" % _h: ("sbuf", [128, 128], "bfloat16"),
+                    "UL%d" % _h: ("sbuf", [128, 128], "float32"), "SQ%d" % _h: ("sbuf", [128, 32], "float32"), "SZ%d" % _h: ("sbuf", [128, 32], "float32"),
+                    "XI%d" % _h: ("sbuf", [128, 32], "int32"), "OF%d" % _h: ("sbuf", [128, 32], "uint16"), "VK%d" % _h: ("sbuf", [128, 32], "float32")})
+for _t in range(TS):
+    SCRATCH.update({"ZF%d" % _t: ("sbuf", [128, 256], "bfloat16"), "ZP%d" % _t: ("sbuf", [128, 256], "bfloat16"), "LQ%d" % _t: ("sbuf", [128, 16], "uint16"),
+                    "RL%d" % _t: ("sbuf", [128, 16], "uint16"), "DO%d" % _t: ("sbuf", [128, 16], "bfloat16"), "DR%d" % _t: ("sbuf", [128, 16], "bfloat16")})
+SEMAPHORES = ["cV", "cS", "cP", "cG", "dx", "dv", "ds", "dt", "dy", "dz", "loc"] + ["r%s%d" % (k, t) for k in "LZD" for t in range(TS)]
+CYC, WAKE, SFIX, LOOK, PUT, REMOTE = 0.00083, 0.06, 0.1, 1.5, 3.8, 2.2
+MARGIN = 3
+GAP = {"S": 0.3, "V": 0.9}
+HITS_ON_VECTOR = (2, 5, 8, 11, 14)
+
+
+def rank_program(g, core, T, topo):
+    rank = T.rank_of(core)
+    if rank is None:
+        return
+    eng = {"V": g.vector, "S": g.scalar, "P": g.tensor, "G": g, "Y": g.sync}
+    ops = []
+    chain = [None]
+
+    def op(q, reads, writes, cost, f, kind="c", sem=None, n=0, lat=0.0):
+        ops.append({"chain": chain[0], "q": q, "r": reads.split(), "w": writes.split(), "cost": cost, "f": f, "kind": kind, "sem": sem, "n": n, "lat": lat})
+
+    def dma(q, sem, total, out, in_, reads, writes):
+        op(q, reads, writes, 0.1, lambda e: e.dma_start(out, in_).then_inc(T.sem[sem], 16), "d", sem, total, 8.0 if sem == "dx" else 2.5)
+
+    def part(k, a, b):
+        for group, buf, w in ((FL, "FL", 16), (IL, "IL", 16), (CM, "CM", 128)):
+            if k in group:
+                o = w * group.index(k)
+                return T[buf][:, o + a:o + b]
+        return T[k][:, a:b]
+
+    def lst(k):
+        return part(k, 0, 16)
+
+    def mat(k):
+        return part(k, 0, 128)
+
+    def vc(n):
+        return max(n, 64) * CYC
+
+    def ts(reads, writes, n, out, in0, s1, o1, s2=None, o2=None):
+        if o2 is None:
+            op("V", reads, writes, vc(n), lambda e: e.tensor_scalar(out, in0, s1, None, o1))
+        else:
+            op("V", reads, writes, vc(n), lambda e: e.tensor_scalar(out, in0, s1, s2, o1, o2))
+
+    def tt(reads, writes, n, out, in0, in1, o):
+        op("V", reads, writes, vc(n), lambda e: e.tensor_tensor(out, in0, in1, o))
+
+    def cp(reads, writes, n, out, in_):
+        op("V", reads, writes, vc(n), lambda e: e.tensor_copy(out, in_))
+
+    def act(reads, writes, n, out, in_, fn, bias=0.0, scale=1.0):
+        op("S", reads, writes, SFIX + n * CYC, lambda e: e.activation(out, in_, fn, bias=bias, scale=scale))
+
+    def mm(reads, writes, n, out, lhsT, rhs, a, z):
+        op("P", reads, writes, vc(n), lambda e: e.matmul(out, lhsT, rhs, a, z))
+
+    def scan(reads, writes, n, out, d0, d1, init, o0, o1):
+        op("V", reads, writes, vc(n), lambda e: e.tensor_tensor_scan(out, d0, d1, init, o0, o1))
+
+    def fill(key, n, ap, c):
+        op("V", "", key, vc(n), lambda e: e.memset(ap, c))
+
+    def iota(key, n, out, pat, base, cm):
+        op("G", "", key, 0.13 + 2 * n * CYC, lambda e: e.iota(out, pat, base, cm, allow_small_or_imprecise_dtypes=True))
+
+    def looks(n):
+        return LOOK * n + 60
+
+    def puts(n):
+        return PUT * n + 60
+    sent = [0]
+
+    def send(t, kind, dst, src, keys):
+        to = T.cores[rank ^ (1 + t % (len(T.cores) - 1))]
+        rid, pid = topo.addr(to)[:2]
+        m = topo.mask(core, to)
+        n = bin(m).count("1")
+        sem = "r%s%d" % (kind, t)
+        sent[0] += n
+        op("G", keys, "recv%s%d" % (kind, t), 0.3, lambda e: e.remote_dma(dst, src, T.sem[sem], T.sem.loc, pid, rid, m), "r", sem, n, REMOTE)
+
+    XK = "Xa Xb"
+    dma("S", "dv", 16, T.V0[:], T.v0[:], "", "V0")
+    dma("S", "ds", 16, T.SD[:], T.sd[:], "", "SD")
+    dma("S", "dt", 16, T.TI[:], T.th[:], "", "TI")
+    dma("Y", "dx", 32, T.X[0:64, 0:W], T.x[0:64, :], "", "Xa")
+    dma("Y", "dx", 32, T.X[64:128, 0:W], T.x[64:128, :], "", "Xb")
+
+    iota("PI0", 1, T.PI[:, 0:1], [[0, 1]], 0, 1)
+    iota("RM", 256, T.RM[:], [[0, 16], [1, 16]], 0, 0)
+    iota("RP", 128, T.RP[:], [[1, 128]], 0, 0)
+    iota("RG", 128, T.RG[:], [[1, 8], [0, 16]], 0, 0)
+    iota("RD", 256, T.RD[:], [[1, 16], [0, 16]], 0, 0)
+    iota("DMI", 16, T.DM[:], [[16, 16]], W, 0)
+    for j in range(16):
+        iota("IO%d" % j, 512, T.IO[:, 512 * j:512 * j + 512], [[1, 512]], 512 * j, 0)
+    IOK = " ".join("IO%d" % j for j in range(16))
+    ts("PI0", "PI1", 1, T.PI[:, 1:2], T.PI[:, 0:1], 15, Op.bitwise_and)
+    ts("PI0", "PI2", 1, T.PI[:, 2:3], T.PI[:, 0:1], 4, Op.arith_shift_right)
+    cp("PI0 PI1 PI2", "PF", 3, T.PF[:, 0:3], T.PI[:, 0:3])
+    p, pi, pg = T.PF[:, 0:1], T.PF[:, 1:2], T.PF[:, 2:3]
+    ts("RM PF", "NM", 256, T.NM[:], T.RM[:], pi, Op.not_equal, -8192.0, Op.mult)
+    ts("RG PF", "BO", 128, mat("BO"), T.RG[:], pg, Op.is_equal)
+    ts("RM", "K4", 256, T.K4[:], T.RM[:], 0.0, Op.is_equal, -16384.0, Op.mult)
+    ts("K4", "D0", 256, T.D0[:], T.K4[:], 8192.0, Op.add)
+    ts("RP PF", "ID", 128, mat("ID"), T.RP[:], p, Op.is_equal)
+    ts("RP PF", "NI", 128, mat("NI"), T.RP[:], p, Op.is_equal, -1.0, Op.mult)
+    ts("RP PF", "N5", 128, mat("N5"), T.RP[:], p, Op.is_equal, -512.0, Op.mult)
+    ts("RM PF", "K1", 256, T.K1[:], T.RM[:], pi, Op.is_equal)
+    ts("RM PF", "K2", 128, T.K2[:, 0:128], T.RM[:, 0:128], pi, Op.is_gt)
+    tt("K2 BO", "TG", 256, mat("TG"), T.K2[:, 0:128], mat("BO"), Op.mult)
+    ts("DMI PF", "DM", 16, T.DM[:], T.DM[:], pi, Op.add)
+    fill("OB", 128, T.OB[:], 1.0)
+    fill("ZB", 128, T.ZB[:], 0.0)
+    fill("ON", 64, mat("ON"), 1.0)
+    fill("SC0", 1, T.SC[:, 0:1], 0.0)
+    fill("THR", 16, lst("THR"), 9.0)
+    fill("FR", 16, lst("FR"), 0.0)
+    cp("TI", "TF", 4, T.TF[:], T.TI[:])
+    ts("RD PF", "K2", 256, T.K2[:], T.RD[:], pi, Op.is_equal, 2.0, Op.mult)
+    tt("K1 K2", "K3", 512, T.K3[:], T.K1[:], T.K2[:], Op.mult)
+    ts("K3", "K3", 256, T.K3[:], T.K3[:], 4194304.0, Op.mult)
+    tt("K1 K3", "K3", 512, T.K3[:], T.K3[:], T.K1[:], Op.add)
+    tt("K2 K3", "CO", 512, T.CO[:], T.K3[:], T.K2[:], Op.add)
+    fill("TH0", 16, T.TH[:, 0:4], 0.75 * 2.0 ** 33)
+    for k in range(1, 4):
+        fill("TH%d" % k, 16, T.TH[:, 4 * k:4 * k + 4], 0.75 * 2.0 ** (11 * (3 - k)))
+    cp("TH0 TH1 TH2 TH3", "TH4", 16, T.TH[:, 16:32], T.TH[:, 0:16])
+    cp("TH0 TH1 TH2 TH3 TH4", "TH5", 32, T.TH[:, 32:64], T.TH[:, 0:32])
+    cp("TH0 TH1 TH2 TH3 TH4 TH5", "TH", 64, T.TH[:, 64:128], T.TH[:, 0:64])
+    ts("K1", "K4", 128, T.K4[:, 0:128], T.K1[:, 0:128], 2.0 ** 46, Op.mult, 1.0, Op.max)
+    tt("K4 TH TH5", "TH", 256, T.TH[:], T.TH[:], T.K4[:, 0:128], Op.mult)
+    ts("BO", "K3", 128, T.K3[:, 0:128], mat("BO"), 0.0, Op.is_equal, 1.0e29, Op.mult)
+    tt("K3 TH", "TH", 256, T.TH[:], T.TH[:], T.K3[:, 0:128], Op.max)
+    for h in range(2):
+        for a in range(2):
+            fill("WH%d%d" % (h, a), 1, T.WH[64 * a:64 * a + 64, h:h + 1], 2.0 ** (11 * (3 - 2 * h - a)))
+    for j in range(0, 8464, 1058):
+        fill("QA" + str(j), 529, T.QA[:, j:j + 1058], 0.0)
+        for i in range(j, j + 1058, 264):
+            n = min(264, j + 1058 - i)
+            act("ZB", "HT" + str(j), n, T.HT[:, i:i + n], T.ZB[:, 0:n], AF.Copy)
+            op("G", "", "QB" + str(j), 0.13 + 2 * n * CYC, lambda e, i=i, n=n: e.iota(T.QB[:, i:i + n], [[0, n]], 0, 0, allow_small_or_imprecise_dtypes=True))
+    tabs = {buf: " ".join(buf + str(j) for j in range(0, 8464, 1058)) for buf in ("QA", "HT", "QB")}
+
+    def hs(h):
+        return slice(128 * h, 128 * h + 128)
+
+    def half(k, h):
+        return part(k, 8 * h, 8 * h + 8)
+
+    def rowsum(h, src, key):
+        u, ul = "pU%d" % h, "UL%d" % h
+        mm("ID NM", u, 128, T[u][:, 0:128], mat("ID"), T.NM[:, 0:128], True, False)
+        mm("BO " + key, u, 128, T[u][:, 0:128], mat("BO"), src, False, True)
+        scan("D0 " + u, ul, 128, T[ul][:], T.D0[:, 0:128], T[u][:, 0:128], -8192.0, Op.min, Op.max)
+
+    def squares(h, dst):
+        for m in range(4):
+            act("UL%d" % h, dst + ".%d" % m, 8, T[dst][:, 8 * m:8 * m + 8], T["UL%d" % h][:, 15::16], AF.Square, bias=2.0 * KAPPA[m], scale=0.25)
+
+    def offsets_of(h, b):
+        sq = ("SQ%d" if b else "SZ%d") % h
+        x, o, a = "XI%d" % h, "OF%d" % h, 128 * h + 32 * b
+        tt(" ".join("%s.%d VK%d.%d" % (sq, m, h, m) for m in range(4)), x, 64, T[x][:], T[sq][:], T["VK%d" % h][:], Op.add)
+        ts(x, "TN%d.%d" % (h, b), 32, T.TN[:, a:a + 32], T[x][:], W - 1, Op.bitwise_and)
+        cp("TN%d.%d" % (h, b), o, 32, T[o][:], T.TN[:, a:a + 32])
+
+    def look(h, m):
+        return T.X[:, 0:W].indirect(T["OF%d" % h][:, 8 * m:8 * m + 8])
+
+    def vk(h):
+        for m in range(4):
+            ts("VN", "VK%d.%d" % (h, m), 8, T["VK%d" % h][:, 8 * m:8 * m + 8], half("VN", h), -4.0 * KAPPA[m] ** 2 - 0.25, Op.add)
+
+    def step(t, b, h):
+        y, a, bb, c, o, d, z = ["%s%d" % (k, h) for k in ("Y", "A", "B", "C", "OF", "pD", "Z")]
+        src, zk = (T.SD[:, hs(h)], "SD") if b == 0 else (T[z][:], z)
+        mm("NI " + zk, d, 128, T[d][:, 0:128], mat("NI"), src, True, False)
+        if b:
+            rowsum(h, T[z][:], z)
+            squares(h, "SQ%d" % h)
+        offsets_of(h, b)
+        act("%s %s" % (XK, o), y, looks(128), T[y][:], look(h, 0), AF.Copy)
+        tt("%s %s %s" % (XK, o, y), a, looks(128), T[a][:], look(h, 1), T[y][:], Op.max)
+        tt("%s %s %s" % (XK, o, a), bb, looks(128), T[bb][:], look(h, 2), T[a][:], Op.max)
+        tt("%s %s %s" % (XK, o, bb), c, looks(128), T[c][:], look(h, 3), T[bb][:], Op.max)
+        mm("ID " + c, d, 128, T[d][:, 0:128], mat("ID"), T[c][:], False, True)
+        if b < 3:
+            act(d, z, 128, T[z][:], T[d][:, 0:128], AF.Abs)
+        else:
+            act(d, "ZF%d.%d" % (t, h), 128, T["ZF%d" % t][:, hs(h)], T[d][:, 0:128], AF.Abs)
+
+    def spread(key, out, src, h):
+        k = "%s%d" % (key, h)
+        act("%s%d" % (src, h), k, 8, out[:, 128 * h:128 * h + 8], half(src, h), AF.Identity, bias=float(D), scale=-float(D))
+        for n in (8, 16, 32, 64):
+            act(k, k, n, out[:, 128 * h + n:128 * h + 2 * n], out[:, 128 * h:128 * h + n], AF.Copy)
+
+    def halts(t, h):
+        f, u = "F%d" % h, "UL%d" % h
+        ts("ZF%d.%d TF" % (t, h), f, 64, T[f][:], T["ZF%d" % t][:, hs(h)], T.TF[:, t:t + 1], Op.is_ge)
+        rowsum(h, T[f][:], f)
+        tt("%s THR" % u, "HA%d" % h, 16, half("HA", h), T[u][:, 15::16], half("THR", h), Op.is_ge)
+        scan("OB HA%d SC%d" % (h, h), "SC%d" % (h + 1), 8, T.SC[:, 1 + 8 * h:9 + 8 * h], T.OB[:, 0:8], half("HA", h), T.SC[:, 8:9] if h else 0.0, Op.mult, Op.add)
+        mm("TG HA%d" % h, "pC", 8, T.pC[:, 8 * h:8 * h + 8], mat("TG"), half("HA", h), True, False)
+        mm("N5 HA%d" % h, "pC", 8, T.pC[:, 8 * h:8 * h + 8], mat("N5"), half("HA", h), False, False)
+        mm("BO SC0 SC1 SC2" if h else "BO SC0 SC1", "pC", 8, T.pC[:, 8 * h:8 * h + 8], mat("BO"), half("SC", h), False, True)
+        ts("pC", "GO%d" % h, 8, half("GO", h), T.pC[:, 8 * h:8 * h + 8], float(CAP - 512), Op.is_lt)
+
+    def shadows(h):
+        for c in range(8 * h, 8 * h + 8):
+            ts("DV VF GO%d" % h, "EB%d" % c, (L - 16 * c) // 2, T.EB[:, c, 0:L - 16 * c], T.DV[:, 16 * c:L], part("VF", c, c + 1), Op.is_equal, part("GO", c, c + 1), Op.mult)
+            mm("TG EB%d" % c, "pH", 16, T.pH[:, 256 + 16 * c:272 + 16 * c], mat("TG"), T.EB[:, c, 0:16], False, c == 15)
+            if c < 15:
+                mm("BO EB%d" % c, "pH", L - 16 - 16 * c, T.pH[:, 272 + 16 * c:512], mat("BO"), T.EB[:, c, 16:L - 16 * c], False, False)
+
+    def places():
+        cp("VN", "OV", 16, T.OV[:], lst("VN"))
+        cp("VN", "VF", 16, lst("VF"), lst("VN"))
+        tt("VF DM", "VD", 32, lst("VD"), lst("VF"), T.DM[:], Op.subtract)
+        cp("OV " + IOK, "DV", looks(256), T.DV[:], T.IO[:].indirect(T.OV[:]))
+
+    def base():
+        ts("VC", "S1", 16, lst("S1"), lst("VC"), 4095, Op.bitwise_and)
+        tt("S1", "S2", 32, lst("S2"), lst("S1"), lst("S1"), Op.mult)
+        ts("S2", "S3", 16, lst("S3"), lst("S2"), 3, Op.arith_shift_right)
+        ts("VC", "S4", 16, lst("S4"), lst("VC"), 37.0, Op.mult)
+        tt("S3 S4", "BA", 32, lst("BA"), lst("S4"), lst("S3"), Op.add)
+
+    def hits(t, onv):
+        cp("OD OB " + tabs["HT"], tabs["HT"], puts(256), T.HT[:, 0:8448].indirect(T.OD[:]), T.OB[:])
+        for k in range(16):
+            h, hb, b0 = k // 8, "HB%d" % (k % 8), 256 * (k % 8)
+            src, key = T.HT[:].indirect(T.OM[:, 16 * k:16 * k + 16]), "%s OM%d" % (tabs["HT"], h)
+            chain[0] = "V" if k in onv else "S"
+            if k in onv:
+                cp(key, hb, looks(256), T.HB[:, b0:b0 + 256], src)
+            else:
+                act(key, hb, looks(256), T.HB[:, b0:b0 + 256], src, AF.Copy)
+            chain[0] = None
+            if k % 8 == 0:
+                mm("ID NM", "pH", 128, T.pH[:, hs(h)], mat("ID"), T.NM[:, 0:128], True, False)
+            for j in range(2):
+                mm("ID " + hb, "pH", 128, T.pH[:, hs(h)], mat("ID"), T.HB[:, b0 + 128 * j:b0 + 128 * j + 128], False, k % 8 == 7 and j == 1)
+        scan("D0 pH", "HUL", 256, T.HUL[:], T.D0[:], T.pH[:, 0:256], -8192.0, Op.min, Op.max)
+        tt("FR recvD%d" % t, "FS", 32, lst("FS"), T["DR%d" % t][:], lst("FR"), Op.add)
+        tt("HUL FS", "FR FR0 FR1", 32, lst("FR"), T.HUL[:, 15::16], lst("FS"), Op.is_lt)
+        tt("VC VN", "S5", 32, lst("S5"), lst("VC"), lst("VN"), Op.subtract)
+        tt("S5 FR", "S6", 32, lst("S6"), lst("S5"), lst("FR"), Op.mult)
+        tt("S6 VN", "VC", 32, lst("VC"), lst("S6"), lst("VN"), Op.add)
+
+    def keep():
+        ts("FR", "THR", 16, lst("THR"), lst("FR"), 1000.0, Op.mult, 9.0, Op.add)
+        base()
+        for h in range(2):
+            spread("NF", T.NF, "FR", h)
+        ts("NF0 NF1", "FO", 128, T.FO[:], T.NF[:], -1.0, Op.mult, float(D), Op.add)
+        tt("TR NF0 NF1", "P1", 512, T.P1[:], T.TR[:], T.NF[:], Op.max)
+
+    def wipe(Q):
+        for j in range(0, 8448, 264):
+            op("G", "", "%s%d" % (Q, j // 1056 * 1058), 0.13 + 528 * CYC, lambda e, j=j: e.iota(T[Q][:, j:j + 264], [[0, 264]], 0, 0, allow_small_or_imprecise_dtypes=True))
+
+    cp("V0", "VN", 16, lst("VN"), T.V0[:])
+    cp("V0", "VC", 16, lst("VC"), T.V0[:])
+    for h in range(2):
+        rowsum(h, T.SD[:, hs(h)], "SD")
+        squares(h, "SZ%d" % h)
+    base()
+
+    for t in range(TS):
+        last = t == TS - 1
+        Q = "QA" if t % 2 == 0 else "QB"
+        zf = "ZF%d" % t
+        vk(0)
+        vk(1)
+        places()
+        for b in range(4):
+            for h in range(2):
+                step(t, b, h)
+        mm("ID NM", "pH", 256, T.pH[:, 256:512], mat("ID"), T.NM[:], True, False)
+        for h in range(2):
+            halts(t, h)
+            shadows(h)
+        if not last:
+            send(t, "Z", T["ZP%d" % t][:], T[zf][:], zf + ".0 " + zf + ".1")
+        scan("D0 pH", "DUL", 256, T.DUL[:], T.D0[:], T.pH[:, 256:512], -8192.0, Op.min, Op.max)
+        tt("DUL GO0 GO1", "OK", 32, lst("OK"), T.DUL[:, 15::16], lst("GO"), Op.is_lt)
+        tt("OK VD", "L1", 32, lst("L1"), lst("VD"), lst("OK"), Op.mult)
+        tt("L1 DM", "L2", 32, lst("L2"), lst("L1"), T.DM[:], Op.add)
+        lq = "LQ%d" % t
+        cp("L2", lq, 16, T[lq][:], lst("L2"))
+        send(t, "L", T["RL%d" % t][:], T[lq][:], lq)
+        for h in range(2):
+            spread("NG", T.NG, "GO", h)
+            tn = " ".join("TN%d.%d" % (h, b) for b in range(4))
+            tt("%s NG%d" % (tn, h), "M1%d" % h, 256, T.M1[:, hs(h)], T.TN[:, hs(h)], T.NG[:, hs(h)], Op.max)
+            if t == 0:
+                cp("M1%d" % h, "OM%d" % h, 128, T.OM[:, hs(h)], T.M1[:, hs(h)])
+            else:
+                tt("M1%d P1" % h, "M2%d" % h, 256, T.M2[:, hs(h)], T.M1[:, hs(h)], T.P1[:, hs(h)], Op.min)
+                cp("M2%d" % h, "OM%d" % h, 128, T.OM[:, hs(h)], T.M2[:, hs(h)])
+        rl = T["RL%d" % t]
+        rk = "recvL%d" % t
+        cp("%s CO %s" % (rk, tabs[Q]), tabs[Q], puts(256), T[Q][:, 0:8448].indirect(rl[:]), T.CO[:])
+        cp(rk, "LF", 16, lst("LF"), rl[:])
+        ts("LF", "IW", 16, lst("IW"), lst("LF"), float(W), Op.is_lt)
+        tt("LF DM", "LD", 32, lst("LD"), lst("LF"), T.DM[:], Op.subtract)
+        tn = " ".join("TN%d.%d" % (h, b) for b in range(4) for h in range(2))
+        if t == 0:
+            cp(tn, "TR", 256, T.TR[:], T.TN[:])
+        else:
+            tt(tn + " FO", "P2", 512, T.P2[:], T.TN[:], T.FO[:], Op.max)
+            tt("P1 P2", "TR", 512, T.TR[:], T.P2[:], T.P1[:], Op.min)
+            cp("OD ZB " + tabs["HT"], tabs["HT"], puts(256), T.HT[:, 0:8448].indirect(T.OD[:]), T.ZB[:, 0:256])
+        if last:
+            for h in range(2):
+                dma("Y", "dz", 32, T.YT[:, :, 8 * h:8 * h + 8], T.TR[:, hs(h)], "TR", "YT%d" % h)
+            dma("Y", "dy", 32, T.yt[:], T.YT[:], "YT0 YT1", "yt")
+
+        def turn(k):
+            b0, pt, a0 = 512 * k, "pT%d" % (k % 2), 512 * (k % 4)
+            for j in range(4):
+                op("P", "ID GB%d%s" % (k, "aabb"[j]), pt, 128 * CYC, lambda e, j=j: e.transpose(T[pt][:, 128 * j:128 * j + 128], T.GB[:, b0 + 128 * j:b0 + 128 * j + 128], mat("ID")))
+            ts("%s WH%d0 WH%d1" % (pt, k // 4, k // 4), "LA%d" % (k % 4), 256, T.LA[:, a0:a0 + 512], T[pt][:, 0:512], T.WH[:, k // 4:k // 4 + 1], Op.mult)
+            ts(pt, "LB%d" % (k % 4), 256, T.LB[:, a0:a0 + 512], T[pt][:, 0:512], -1.0, Op.add, 0.0, Op.max)
+
+        def cells(k):
+            for j in range(4):
+                a0 = 512 * (k % 4) + 128 * j
+                mm("LA%d LB%d" % (k % 4, k % 4), "pC", 128, T.pC[:, 128:256], T.LA[:, a0:a0 + 128], T.LB[:, a0:a0 + 128], k == 0 and j == 0, k == 7 and j == 3)
+        for k in range(8):
+            key = "%s OM%d" % (tabs[Q], k // 4)
+            if k == 0:
+                cp(key, "GB0a", looks(256), T.GB[:, 0:256], T[Q][:].indirect(T.OM[:, 0:16]))
+                act(key, "GB0b", looks(256), T.GB[:, 256:512], T[Q][:].indirect(T.OM[:, 16:32]), AF.Copy)
+            else:
+                act(key, "GB%da GB%db" % (k, k), looks(512), T.GB[:, 512 * k:512 * k + 512], T[Q][:].indirect(T.OM[:, 32 * k:32 * k + 32]), AF.Copy)
+        for k in range(8):
+            turn(k)
+            cells(k)
+        tt("pC TH", "MC", 128, T.MC[:], T.pC[:, 128:256], T.TH[:], Op.is_ge)
+        tt("MC", "MD", 128, T.MD[:], T.MC[:, 0:64], T.MC[:, 64:128], Op.add)
+        tt("MD", "ME", 64, T.ME[:], T.MD[:, 0:32], T.MD[:, 32:64], Op.add)
+        tt("ME", "MF", 32, T.MF[:], T.ME[:, 0:16], T.ME[:, 16:32], Op.add)
+        do = "DO%d" % t
+        tt("MF IW", do, 32, T[do][:], T.MF[:], lst("IW"), Op.is_lt)
+        mm("ON " + do, "pC", 16, T.pC[:, 0:16], mat("ON"), T[do][:], True, True)
+        send(t, "D", T["DR%d" % t][:], T[do][:], do)
+        tt("LD " + do, "E1", 32, lst("E1"), lst("LD"), T[do][:], Op.mult)
+        tt("E1 DM", "E2", 32, lst("E2"), lst("E1"), T.DM[:], Op.add)
+        cp("E2", "OD", 16, T.OD[:], lst("E2"))
+        op("V", "pC", "AA", vc(16), lambda e: e.tensor_reduce(T.AA[:], T.pC[:, 0:16], AxisListType.X, Op.add))
+        if not last:
+            cp("OD recvZ%d" % t, XK, puts(256), T.X[:].indirect(T.OD[:]), T["ZP%d" % t][:])
+        ts("BA AA", "S7", 16, lst("S7"), lst("BA"), T.AA[:], Op.add)
+        ts("S7", "VN", 16, lst("VN"), lst("S7"), W - 1, Op.bitwise_and)
+        if t < 2:
+            wipe(Q)
+        hits(t, (1, 3, 5, 7, 9, 11, 13, 15) if last else HITS_ON_VECTOR)
+        if not last:
+            keep()
+    cp("VC", "YS", 16, T.YS[:, 0:16], lst("VC"))
+    cp("FR", "YS", 16, T.YS[:, 16:32], lst("FR"))
+    dma("Y", "dy", 32, T.ys[:], T.YS[:], "YS", "ys")
+
+    N = len(ops)
+    preds = [dict() for _ in ops]
+    last_w, readers, banks = {}, {}, {}
+    ends = {}
+    for i, o in enumerate(ops):
+        def after(j, wake):
+            if j != i:
+                preds[i][j] = max(preds[i].get(j, 0.0), wake)
+        if o["chain"]:
+            if o["chain"] in ends:
+                after(ends[o["chain"]], 0.0)
+            ends[o["chain"]] = i
+        for k in o["r"] + o["w"]:
+            if k[0] == "p":
+                for q, j in banks.get(k, {}).items():
+                    after(j, WAKE if q != o["q"] else 0.0)
+        for k in o["r"]:
+            if k[0] != "p" and k in last_w:
+                after(last_w[k], WAKE)
+        for k in o["w"]:
+            if k[0] != "p":
+                if k in last_w:
+                    after(last_w[k], WAKE)
+                for j in readers.get(k, []):
+                    after(j, WAKE if ops[j]["q"] != o["q"] else 0.0)
+        for k in o["r"] + o["w"]:
+            if k[0] == "p":
+                banks.setdefault(k, {})[o["q"]] = i
+        for k in o["r"]:
+            if k[0] != "p":
+                readers.setdefault(k, []).append(i)
+        for k in o["w"]:
+            if k[0] != "p":
+                last_w[k] = i
+                readers[k] = []
+    succs = [[] for _ in ops]
+    for i in range(N):
+        for j, wake in preds[i].items():
+            succs[j].append((i, wake))
+    prio = [0.0] * N
+    for i in range(N - 1, -1, -1):
+        best = 0.0
+        for j, wake in succs[i]:
+            gap = GAP[ops[i]["chain"]] if ops[i]["chain"] and ops[i]["chain"] == ops[j]["chain"] else 0.0
+            best = max(best, wake + ops[i]["lat"] + gap + prio[j])
+        prio[i] = best + ops[i]["cost"]
+    left = [len(preds[i]) for i in range(N)]
+    ready = [0.0] * N
+    free = {q: 0.0 for q in eng}
+    avail = {q: [] for q in eng}
+    for i in range(N):
+        if left[i] == 0:
+            avail[ops[i]["q"]].append(i)
+    order = []
+    over = [False] * N
+    came = [0.0] * N
+    line = {q: sorted((i for i in range(N) if ops[i]["q"] == q), key=lambda i: -prio[i]) for q in eng}
+
+    def soonest(i, memo):
+        if left[i] == 0:
+            return ready[i]
+        if i not in memo:
+            best = 0.0
+            for j, wake in preds[i].items():
+                if over[j]:
+                    best = max(best, came[j] + ops[j]["lat"] + wake)
+                else:
+                    best = max(best, max(soonest(j, memo), free[ops[j]["q"]]) + ops[j]["cost"] + ops[j]["lat"] + wake)
+            memo[i] = best
+        return memo[i]
+
+    while len(order) < N:
+        pick = None
+        for q in "VSPGY":
+            if avail[q]:
+                t0 = max(free[q], min(ready[i] for i in avail[q]))
+                if pick is None or t0 < pick[0]:
+                    pick = (t0, q)
+        t0, q = pick
+        line[q] = [i for i in line[q] if not over[i]]
+        memo, i, wait = {}, None, None
+        for c in sorted((c for c in avail[q] if ready[c] <= t0), key=lambda c: -prio[c]):
+            cost = ops[c]["cost"]
+            block = None
+            for j in line[q][:8]:
+                if j == c or prio[j] < prio[c] + MARGIN * cost:
+                    break
+                e = soonest(j, memo)
+                if t0 < e < t0 + cost - 0.02:
+                    block = e if block is None else min(block, e)
+            if block is None:
+                i = c
+                break
+            wait = block if wait is None else min(wait, block)
+        if i is None:
+            free[q] = wait
+            continue
+        avail[q].remove(i)
+        done = t0 + ops[i]["cost"]
+        free[q] = came[i] = done
+        over[i] = True
+        order.append(i)
+        for j, wake in succs[i]:
+            ready[j] = max(ready[j], done + ops[i]["lat"] + wake)
+            left[j] -= 1
+            if left[j] == 0:
+                avail[ops[j]["q"]].append(j)
+
+    count = {q: 0 for q in eng}
+    clock = {q: {} for q in eng}
+    wr, rd, bank = {}, {}, {}
+
+    def need(q, tok):
+        s, n, known = tok
+        if clock[q].get(s, 0) < n:
+            eng[q].wait_ge(T.sem[s], n)
+            clock[q][s] = n
+            for k, m in known.items():
+                clock[q][k] = max(clock[q].get(k, 0), m)
+
+    for i in order:
+        o = ops[i]
+        q, keys = o["q"], o["r"] + o["w"]
+        toks = []
+        for k in keys:
+            if k[0] == "p":
+                toks += [tok for q2, tok in bank.get(k, {}).items() if q2 != q]
+            elif k in wr:
+                toks.append(wr[k])
+        for k in o["w"]:
+            if k[0] != "p":
+                toks += [tok for q2, tok in rd.get(k, {}).items() if q2 != q]
+        best = {}
+        for tok in toks:
+            if tok[0] not in best or best[tok[0]][1] < tok[1]:
+                best[tok[0]] = tok
+        for s in sorted(best, key=lambda s: -len(best[s][2])):
+            need(q, best[s])
+        ins = o["f"](eng[q])
+        if o["kind"] == "c":
+            ins.then_inc(T.sem["c" + q], 1)
+            count[q] += 1
+            tok = ("c" + q, count[q], dict(clock[q]))
+        elif o["kind"] == "d":
+            tok = (o["sem"], o["n"], dict(clock[q]))
+        else:
+            tok = (o["sem"], o["n"], {})
+        for k in keys:
+            if k[0] == "p":
+                bank.setdefault(k, {})[q] = tok
+        for k in o["r"]:
+            if k[0] != "p" and o["kind"] != "r":
+                rd.setdefault(k, {})[q] = tok
+        for k in o["w"]:
+            if k[0] != "p":
+                wr[k] = tok
+                rd[k] = {}
+    g.sync.wait_ge(T.sem.dy, 32)
+    g.wait_ge(T.sem.loc, sent[0])
+    for q in "VSPG":
+        g.wait_ge(T.sem["c" + q], count[q])

@@ -3,9 +3,9 @@ from concourse.mybir import AluOpType as Op, AxisListType, ActivationFunctionTyp
 W, L, D = 8192, 256, 8448
 KAPPA = (3, 29, 71, 113)
 TS, CAP = 4, 128
-FL = "GO THR OK L1 L2 LF IW LD E1 E2 FR FS VF VD BA S4 S5 S6".split()
+FL = "GO THR DS L1 L2 LF IW LD E1 E2 FR FS VF BA S4 S5 S6".split()
 IL = "VN VC S1 S2 S3 S7".split()
-CM = "ID NI N5 BO TG ON".split()
+CM = "ID NI N5 BO TG ON BK TK".split()
 
 SCRATCH = {
     "X": ("sbuf", [128, 8448], "bfloat16"),
@@ -16,6 +16,7 @@ SCRATCH = {
     "RM": ("sbuf", [128, 256], "float32"), "RD": ("sbuf", [128, 256], "float32"), "RP": ("sbuf", [128, 128], "float32"), "RG": ("sbuf", [128, 128], "float32"),
     "K1": ("sbuf", [128, 256], "float32"), "K2": ("sbuf", [128, 256], "float32"), "K3": ("sbuf", [128, 256], "float32"), "K4": ("sbuf", [128, 256], "float32"),
     "CM": ("sbuf", [128, 128 * len(CM)], "bfloat16"), "FL": ("sbuf", [128, 16 * len(FL)], "float32"), "IL": ("sbuf", [128, 16 * len(IL)], "int32"),
+    "KA": ("sbuf", [128, 256], "float32"), "KC": ("sbuf", [128, 256], "float32"), "NK": ("sbuf", [128, 256], "bfloat16"),
     "NM": ("sbuf", [128, 256], "bfloat16"), "CO": ("sbuf", [128, 256], "bfloat16"), "D0": ("sbuf", [128, 256], "float32"),
     "TH": ("sbuf", [128, 128], "float32"), "WH": ("sbuf", [128, 2], "float32"), "DM": ("sbuf", [128, 16], "float32"),
     "OB": ("sbuf", [128, 256], "bfloat16"), "ZB": ("sbuf", [128, 264], "bfloat16"),
@@ -28,21 +29,21 @@ SCRATCH = {
     "MC": ("sbuf", [128, 128], "bfloat16"), "MD": ("sbuf", [128, 64], "bfloat16"), "ME": ("sbuf", [128, 32], "bfloat16"), "MF": ("sbuf", [128, 16], "bfloat16"),
     "AA": ("sbuf", [128, 1], "float32"), "YT": ("sbuf", [128, 16, 16], "float32"), "YS": ("sbuf", [128, 32], "float32"),
     "GB": ("sbuf", [128, 4096], "bfloat16"), "HB": ("sbuf", [128, 2048], "bfloat16"), "LA": ("sbuf", [128, 2048], "bfloat16"), "LB": ("sbuf", [128, 2048], "bfloat16"),
-    "pU0": ("psum", [128, 512], "float32"), "pU1": ("psum", [128, 512], "float32"), "pD0": ("psum", [128, 512], "float32"), "pD1": ("psum", [128, 512], "float32"),
+    "pU": ("psum", [128, 512], "float32"), "pD0": ("psum", [128, 512], "float32"), "pD1": ("psum", [128, 512], "float32"),
     "pT0": ("psum", [128, 1024], "bfloat16"), "pT1": ("psum", [128, 1024], "bfloat16"), "pC": ("psum", [128, 512], "float32"), "pH": ("psum", [128, 512], "float32"),
 }
-for _h in range(2):
-    SCRATCH.update({"Z%d" % _h: ("sbuf", [128, 128], "bfloat16"), "Y%d" % _h: ("sbuf", [128, 128], "bfloat16"), "A%d" % _h: ("sbuf", [128, 128], "bfloat16"),
-                    "B%d" % _h: ("sbuf", [128, 128], "bfloat16"), "C%d" % _h: ("sbuf", [128, 128], "bfloat16"), "F%d" % _h: ("sbuf", [128, 128], "bfloat16"),
-                    "UL%d" % _h: ("sbuf", [128, 128], "float32"), "SQ%d" % _h: ("sbuf", [128, 32], "float32"), "SZ%d" % _h: ("sbuf", [128, 32], "float32"),
-                    "XI%d" % _h: ("sbuf", [128, 32], "int32"), "OF%d" % _h: ("sbuf", [128, 32], "uint16"), "VK%d" % _h: ("sbuf", [128, 32], "float32")})
+SCRATCH.update({"Z": ("sbuf", [128, 256], "bfloat16"), "Y": ("sbuf", [128, 1024], "bfloat16"), "F": ("sbuf", [128, 256], "bfloat16"),
+                "UL": ("sbuf", [128, 256], "float32"), "SQ": ("sbuf", [128, 64], "float32"), "SZ": ("sbuf", [128, 64], "float32"), "XQ": ("sbuf", [128, 32], "float32"),
+                "XI": ("sbuf", [128, 64], "int32"), "OF": ("sbuf", [128, 64], "uint16"), "VK": ("sbuf", [128, 64], "float32")})
 for _t in range(TS):
     SCRATCH.update({"ZF%d" % _t: ("sbuf", [128, 256], "bfloat16"), "ZP%d" % _t: ("sbuf", [128, 256], "bfloat16"), "LQ%d" % _t: ("sbuf", [128, 16], "uint16"),
                     "RL%d" % _t: ("sbuf", [128, 16], "uint16"), "DO%d" % _t: ("sbuf", [128, 16], "bfloat16"), "DR%d" % _t: ("sbuf", [128, 16], "bfloat16")})
 SEMAPHORES = ["cV", "cS", "cP", "cG", "dx", "dv", "ds", "dt", "dy", "dz", "loc"] + ["r%s%d" % (k, t) for k in "LZD" for t in range(TS)]
-CYC, WAKE, SFIX, LOOK, PUT, REMOTE = 0.00083, 0.06, 0.1, 1.5, 3.8, 2.2
+CYC, WAKE, SFIX, LOOK, PUT, REMOTE = 0.00083, 0.15, 0.15, 1.3, 3.0, 3.0
 MARGIN = 3
+SFIRST = (1,)
 GAP = {"S": 0.3, "V": 0.9}
+POS = (0, 256, 128, 384)
 HITS_ON_VECTOR = (2, 5, 8, 11, 14)
 
 
@@ -58,7 +59,7 @@ def rank_program(g, core, T, topo):
         ops.append({"chain": chain[0], "q": q, "r": reads.split(), "w": writes.split(), "cost": cost, "f": f, "kind": kind, "sem": sem, "n": n, "lat": lat})
 
     def dma(q, sem, total, out, in_, reads, writes):
-        op(q, reads, writes, 0.1, lambda e: e.dma_start(out, in_).then_inc(T.sem[sem], 16), "d", sem, total, 8.0 if sem == "dx" else 2.5)
+        op(q, reads, writes, 0.1, lambda e: e.dma_start(out, in_).then_inc(T.sem[sem], 16), "d", sem, total, 7.0 if sem == "dx" else 2.5)
 
     def part(k, a, b):
         for group, buf, w in ((FL, "FL", 16), (IL, "IL", 16), (CM, "CM", 128)):
@@ -74,7 +75,7 @@ def rank_program(g, core, T, topo):
         return part(k, 0, 128)
 
     def vc(n):
-        return max(n, 64) * CYC
+        return 0.02 + max(n, 64) * CYC
 
     def ts(reads, writes, n, out, in0, s1, o1, s2=None, o2=None):
         if o2 is None:
@@ -132,8 +133,9 @@ def rank_program(g, core, T, topo):
     iota("RG", 128, T.RG[:], [[1, 8], [0, 16]], 0, 0)
     iota("RD", 256, T.RD[:], [[1, 16], [0, 16]], 0, 0)
     iota("DMI", 16, T.DM[:], [[16, 16]], W, 0)
-    for j in range(16):
+    for j in range(8):
         iota("IO%d" % j, 512, T.IO[:, 512 * j:512 * j + 512], [[1, 512]], 512 * j, 0)
+        act("IO%d" % j, "IO%d" % (j + 8), 512, T.IO[:, 512 * j + 4096:512 * j + 4608], T.IO[:, 512 * j:512 * j + 512], AF.Identity, bias=4096.0)
     IOK = " ".join("IO%d" % j for j in range(16))
     ts("PI0", "PI1", 1, T.PI[:, 1:2], T.PI[:, 0:1], 15, Op.bitwise_and)
     ts("PI0", "PI2", 1, T.PI[:, 2:3], T.PI[:, 0:1], 4, Op.arith_shift_right)
@@ -141,15 +143,22 @@ def rank_program(g, core, T, topo):
     p, pi, pg = T.PF[:, 0:1], T.PF[:, 1:2], T.PF[:, 2:3]
     ts("RM PF", "NM", 256, T.NM[:], T.RM[:], pi, Op.not_equal, -8192.0, Op.mult)
     ts("RG PF", "BO", 128, mat("BO"), T.RG[:], pg, Op.is_equal)
-    ts("RM", "K4", 256, T.K4[:], T.RM[:], 0.0, Op.is_equal, -16384.0, Op.mult)
-    ts("K4", "D0", 256, T.D0[:], T.K4[:], 8192.0, Op.add)
+    ts("RM", "K4", 256, T.K4[:], T.RM[:], 0.0, Op.is_equal, -65536.0, Op.mult)
+    ts("K4", "D0", 256, T.D0[:], T.K4[:], 32768.0, Op.add)
     ts("RP PF", "ID", 128, mat("ID"), T.RP[:], p, Op.is_equal)
     ts("RP PF", "NI", 128, mat("NI"), T.RP[:], p, Op.is_equal, -1.0, Op.mult)
     ts("RP PF", "N5", 128, mat("N5"), T.RP[:], p, Op.is_equal, -512.0, Op.mult)
     ts("RM PF", "K1", 256, T.K1[:], T.RM[:], pi, Op.is_equal)
     ts("RM PF", "K2", 128, T.K2[:, 0:128], T.RM[:, 0:128], pi, Op.is_gt)
     tt("K2 BO", "TG", 256, mat("TG"), T.K2[:, 0:128], mat("BO"), Op.mult)
+    ts("BO", "BK", 128, mat("BK"), mat("BO"), 32768.0, Op.mult)
+    ts("ID", "KA", 128, T.KA[:, 0:128], mat("ID"), -16384.0, Op.mult)
+    ts("TG", "KB", 128, T.KA[:, 128:256], mat("TG"), 32768.0, Op.mult)
+    tt("KA KB", "TK", 256, mat("TK"), T.KA[:, 0:128], T.KA[:, 128:256], Op.add)
+    ts("RM PF", "KC", 256, T.KC[:], T.RM[:], pi, Op.not_equal, -float(2 ** 24 + 2 ** 14), Op.mult)
+    ts("KC", "NK", 256, T.NK[:], T.KC[:], 16384.0, Op.add)
     ts("DMI PF", "DM", 16, T.DM[:], T.DM[:], pi, Op.add)
+    ts("DM", "DS", 16, lst("DS"), T.DM[:], 1.0 / 16384, Op.mult)
     fill("OB", 128, T.OB[:], 1.0)
     fill("ZB", 128, T.ZB[:], 0.0)
     fill("ON", 64, mat("ON"), 1.0)
@@ -175,90 +184,93 @@ def rank_program(g, core, T, topo):
     for h in range(2):
         for a in range(2):
             fill("WH%d%d" % (h, a), 1, T.WH[64 * a:64 * a + 64, h:h + 1], 2.0 ** (11 * (3 - 2 * h - a)))
+    pieces = []
     for j in range(0, 8464, 1058):
         fill("QA" + str(j), 529, T.QA[:, j:j + 1058], 0.0)
         for i in range(j, j + 1058, 264):
             n = min(264, j + 1058 - i)
             act("ZB", "HT" + str(j), n, T.HT[:, i:i + n], T.ZB[:, 0:n], AF.Copy)
-            op("G", "", "QB" + str(j), 0.13 + 2 * n * CYC, lambda e, i=i, n=n: e.iota(T.QB[:, i:i + n], [[0, n]], 0, 0, allow_small_or_imprecise_dtypes=True))
+            pieces.append((str(j), i, n))
+
+    def wipe(Q, a, b, behind):
+        for key, i, n in pieces[a:b]:
+            op("G", behind, Q + key, 0.13 + 2 * n * CYC, lambda e, i=i, n=n: e.iota(T[Q][:, i:i + n], [[0, n]], 0, 0, allow_small_or_imprecise_dtypes=True))
     tabs = {buf: " ".join(buf + str(j) for j in range(0, 8464, 1058)) for buf in ("QA", "HT", "QB")}
 
     def hs(h):
         return slice(128 * h, 128 * h + 128)
 
-    def half(k, h):
-        return part(k, 8 * h, 8 * h + 8)
+    def rowsum(src, key0, key1):
+        mm("ID NM", "pU", 256, T.pU[:, 0:256], mat("ID"), T.NM[:], True, False)
+        mm("BO " + key0, "pU", 128, T.pU[:, 0:128], mat("BO"), src[:, 0:128], False, False)
+        mm("BO " + key1, "pU", 128, T.pU[:, 128:256], mat("BO"), src[:, 128:256], False, True)
+        scan("D0 pU", "UL", 256, T.UL[:], T.D0[:], T.pU[:, 0:256], -8192.0, Op.min, Op.max)
 
-    def rowsum(h, src, key):
-        u, ul = "pU%d" % h, "UL%d" % h
-        mm("ID NM", u, 128, T[u][:, 0:128], mat("ID"), T.NM[:, 0:128], True, False)
-        mm("BO " + key, u, 128, T[u][:, 0:128], mat("BO"), src, False, True)
-        scan("D0 " + u, ul, 128, T[ul][:], T.D0[:, 0:128], T[u][:, 0:128], -8192.0, Op.min, Op.max)
+    def squares(dst):
+        for m in range(2):
+            act("UL", "%s.%d" % (dst, m), 16, T[dst][:, 16 * m:16 * m + 16], T.UL[:, 15::16], AF.Square, bias=2.0 * KAPPA[m], scale=0.25)
+        for m in (2, 3):
+            ts("UL", "XQ%d" % m, 16, T.XQ[:, 16 * m - 32:16 * m - 16], T.UL[:, 15::16], 0.25, Op.mult, 2.0 * KAPPA[m], Op.add)
+        tt("XQ2 XQ3", "%s.2" % dst, 64, T[dst][:, 32:64], T.XQ[:], T.XQ[:], Op.mult)
 
-    def squares(h, dst):
+    def vk():
         for m in range(4):
-            act("UL%d" % h, dst + ".%d" % m, 8, T[dst][:, 8 * m:8 * m + 8], T["UL%d" % h][:, 15::16], AF.Square, bias=2.0 * KAPPA[m], scale=0.25)
+            ts("VN", "VK%d" % m, 16, T.VK[:, 16 * m:16 * m + 16], lst("VN"), -4.0 * KAPPA[m] ** 2 - 0.25, Op.add)
 
-    def offsets_of(h, b):
-        sq = ("SQ%d" if b else "SZ%d") % h
-        x, o, a = "XI%d" % h, "OF%d" % h, 128 * h + 32 * b
-        tt(" ".join("%s.%d VK%d.%d" % (sq, m, h, m) for m in range(4)), x, 64, T[x][:], T[sq][:], T["VK%d" % h][:], Op.add)
-        ts(x, "TN%d.%d" % (h, b), 32, T.TN[:, a:a + 32], T[x][:], W - 1, Op.bitwise_and)
-        cp("TN%d.%d" % (h, b), o, 32, T[o][:], T.TN[:, a:a + 32])
-
-    def look(h, m):
-        return T.X[:, 0:W].indirect(T["OF%d" % h][:, 8 * m:8 * m + 8])
-
-    def vk(h):
-        for m in range(4):
-            ts("VN", "VK%d.%d" % (h, m), 8, T["VK%d" % h][:, 8 * m:8 * m + 8], half("VN", h), -4.0 * KAPPA[m] ** 2 - 0.25, Op.add)
-
-    def step(t, b, h):
-        y, a, bb, c, o, d, z = ["%s%d" % (k, h) for k in ("Y", "A", "B", "C", "OF", "pD", "Z")]
-        src, zk = (T.SD[:, hs(h)], "SD") if b == 0 else (T[z][:], z)
-        mm("NI " + zk, d, 128, T[d][:, 0:128], mat("NI"), src, True, False)
+    def step(t, b):
         if b:
-            rowsum(h, T[z][:], z)
-            squares(h, "SQ%d" % h)
-        offsets_of(h, b)
-        act("%s %s" % (XK, o), y, looks(128), T[y][:], look(h, 0), AF.Copy)
-        tt("%s %s %s" % (XK, o, y), a, looks(128), T[a][:], look(h, 1), T[y][:], Op.max)
-        tt("%s %s %s" % (XK, o, a), bb, looks(128), T[bb][:], look(h, 2), T[a][:], Op.max)
-        tt("%s %s %s" % (XK, o, bb), c, looks(128), T[c][:], look(h, 3), T[bb][:], Op.max)
-        mm("ID " + c, d, 128, T[d][:, 0:128], mat("ID"), T[c][:], False, True)
-        if b < 3:
-            act(d, z, 128, T[z][:], T[d][:, 0:128], AF.Abs)
-        else:
-            act(d, "ZF%d.%d" % (t, h), 128, T["ZF%d" % t][:, hs(h)], T[d][:, 0:128], AF.Abs)
+            rowsum(T.Z, "Z0", "Z1")
+            squares("SQ")
+        for h in range(2):
+            src, zk = (T.SD[:, hs(h)], "SD") if b == 0 else (T.Z[:, hs(h)], "Z%d" % h)
+            mm("NI " + zk, "pD%d" % h, 128, T["pD%d" % h][:, 0:128], mat("NI"), src, True, False)
+        sq = "SQ" if b else "SZ"
+        tn = "TN%d" % b
+        tt("%s.0 %s.1 %s.2 VK0 VK1 VK2 VK3" % (sq, sq, sq), "XI", 128, T.XI[:], T[sq][:], T.VK[:], Op.add)
+        ts("XI", tn, 64, T.TN[:, 64 * b:64 * b + 64], T.XI[:], W - 1, Op.bitwise_and)
+        cp(tn, "OF", 64, T.OF[:], T.TN[:, 64 * b:64 * b + 64])
+        for h in range(2):
+            look = [T.X[:, 0:W].indirect(T.OF[:, 16 * m + 8 * h:16 * m + 8 * h + 8]) for m in range(4)]
+            y, d = "Y%d." % h, "pD%d" % h
+            ys = [T.Y[:, 256 * m + 128 * h:256 * m + 128 * h + 128] for m in range(4)]
+            if h in SFIRST:
+                act(XK + " OF", y + "0", looks(128), ys[0], look[0], AF.Copy)
+            else:
+                cp(XK + " OF", y + "0", looks(128), ys[0], look[0])
+            for m in range(1, 4):
+                tt("%s OF %s%d" % (XK, y, m - 1), "%s%d" % (y, m), looks(128), ys[m], look[m], ys[m - 1], Op.max)
+            mm("ID %s3" % y, d, 128, T[d][:, 0:128], mat("ID"), ys[3], False, True)
+            if b < 3:
+                act(d, "Z%d" % h, 128, T.Z[:, hs(h)], T[d][:, 0:128], AF.Abs)
+            else:
+                act(d, "ZF%d.%d" % (t, h), 128, T["ZF%d" % t][:, hs(h)], T[d][:, 0:128], AF.Abs)
 
-    def spread(key, out, src, h):
-        k = "%s%d" % (key, h)
-        act("%s%d" % (src, h), k, 8, out[:, 128 * h:128 * h + 8], half(src, h), AF.Identity, bias=float(D), scale=-float(D))
-        for n in (8, 16, 32, 64):
-            act(k, k, n, out[:, 128 * h + n:128 * h + 2 * n], out[:, 128 * h:128 * h + n], AF.Copy)
+    def spread(key, out, src):
+        act(src, key, 16, out[:, 0:16], lst(src), AF.Identity, bias=float(D), scale=-float(D))
+        for n in (16, 32, 64, 128):
+            act(key, key, n, out[:, n:2 * n], out[:, 0:n], AF.Copy)
 
-    def halts(t, h):
-        f, u = "F%d" % h, "UL%d" % h
-        ts("ZF%d.%d TF" % (t, h), f, 64, T[f][:], T["ZF%d" % t][:, hs(h)], T.TF[:, t:t + 1], Op.is_ge)
-        rowsum(h, T[f][:], f)
-        tt("%s THR" % u, "HA%d" % h, 16, half("HA", h), T[u][:, 15::16], half("THR", h), Op.is_ge)
-        scan("OB HA%d SC%d" % (h, h), "SC%d" % (h + 1), 8, T.SC[:, 1 + 8 * h:9 + 8 * h], T.OB[:, 0:8], half("HA", h), T.SC[:, 8:9] if h else 0.0, Op.mult, Op.add)
-        mm("TG HA%d" % h, "pC", 8, T.pC[:, 8 * h:8 * h + 8], mat("TG"), half("HA", h), True, False)
-        mm("N5 HA%d" % h, "pC", 8, T.pC[:, 8 * h:8 * h + 8], mat("N5"), half("HA", h), False, False)
-        mm("BO SC0 SC1 SC2" if h else "BO SC0 SC1", "pC", 8, T.pC[:, 8 * h:8 * h + 8], mat("BO"), half("SC", h), False, True)
-        ts("pC", "GO%d" % h, 8, half("GO", h), T.pC[:, 8 * h:8 * h + 8], float(CAP - 512), Op.is_lt)
+    def halts(t):
+        for h in range(2):
+            ts("ZF%d.%d TF" % (t, h), "F%d" % h, 64, T.F[:, hs(h)], T["ZF%d" % t][:, hs(h)], T.TF[:, t:t + 1], Op.is_ge)
+        rowsum(T.F, "F0", "F1")
+        tt("UL THR", "HA", 32, T.HA[:], T.UL[:, 15::16], lst("THR"), Op.is_ge)
+        mm("TG HA", "pC", 16, T.pC[:, 0:16], mat("TG"), T.HA[:], True, False)
+        mm("N5 HA", "pC", 16, T.pC[:, 0:16], mat("N5"), T.HA[:], False, False)
+        scan("OB HA", "SC1", 16, T.SC[:, 1:17], T.OB[:, 0:16], T.HA[:], 0.0, Op.mult, Op.add)
+        mm("BO SC0 SC1", "pC", 16, T.pC[:, 0:16], mat("BO"), T.SC[:, 0:16], False, True)
+        ts("pC", "GO", 16, lst("GO"), T.pC[:, 0:16], float(CAP - 512), Op.is_lt)
 
-    def shadows(h):
-        for c in range(8 * h, 8 * h + 8):
-            ts("DV VF GO%d" % h, "EB%d" % c, (L - 16 * c) // 2, T.EB[:, c, 0:L - 16 * c], T.DV[:, 16 * c:L], part("VF", c, c + 1), Op.is_equal, part("GO", c, c + 1), Op.mult)
-            mm("TG EB%d" % c, "pH", 16, T.pH[:, 256 + 16 * c:272 + 16 * c], mat("TG"), T.EB[:, c, 0:16], False, c == 15)
+    def shadows():
+        for c in range(16):
+            ts("DV VF GO", "EB%d" % c, (L - 16 * c) // 2, T.EB[:, c, 0:L - 16 * c], T.DV[:, 16 * c:L], part("VF", c, c + 1), Op.is_equal, part("GO", c, c + 1), Op.mult)
+            mm("TK EB%d" % c, "pH", 16, T.pH[:, 256 + 16 * c:272 + 16 * c], mat("TK"), T.EB[:, c, 0:16], False, c == 15)
             if c < 15:
-                mm("BO EB%d" % c, "pH", L - 16 - 16 * c, T.pH[:, 272 + 16 * c:512], mat("BO"), T.EB[:, c, 16:L - 16 * c], False, False)
+                mm("BK EB%d" % c, "pH", L - 16 - 16 * c, T.pH[:, 272 + 16 * c:512], mat("BK"), T.EB[:, c, 16:L - 16 * c], False, False)
 
     def places():
         cp("VN", "OV", 16, T.OV[:], lst("VN"))
         cp("VN", "VF", 16, lst("VF"), lst("VN"))
-        tt("VF DM", "VD", 32, lst("VD"), lst("VF"), T.DM[:], Op.subtract)
         cp("OV " + IOK, "DV", looks(256), T.DV[:], T.IO[:].indirect(T.OV[:]))
 
     def base():
@@ -271,21 +283,20 @@ def rank_program(g, core, T, topo):
     def hits(t, onv):
         cp("OD OB " + tabs["HT"], tabs["HT"], puts(256), T.HT[:, 0:8448].indirect(T.OD[:]), T.OB[:])
         for k in range(16):
-            h, hb, b0 = k // 8, "HB%d" % (k % 8), 256 * (k % 8)
-            src, key = T.HT[:].indirect(T.OM[:, 16 * k:16 * k + 16]), "%s OM%d" % (tabs["HT"], h)
+            hb, b0 = "HB%d" % (k % 8), 256 * (k % 8)
+            src, key = T.HT[:].indirect(T.OM[:, 16 * k:16 * k + 16]), "%s OM" % tabs["HT"]
             chain[0] = "V" if k in onv else "S"
             if k in onv:
                 cp(key, hb, looks(256), T.HB[:, b0:b0 + 256], src)
             else:
                 act(key, hb, looks(256), T.HB[:, b0:b0 + 256], src, AF.Copy)
             chain[0] = None
-            if k % 8 == 0:
-                mm("ID NM", "pH", 128, T.pH[:, hs(h)], mat("ID"), T.NM[:, 0:128], True, False)
-            for j in range(2):
-                mm("ID " + hb, "pH", 128, T.pH[:, hs(h)], mat("ID"), T.HB[:, b0 + 128 * j:b0 + 128 * j + 128], False, k % 8 == 7 and j == 1)
+            if k == 0:
+                mm("ID NM", "pH", 256, T.pH[:, 0:256], mat("ID"), T.NM[:], True, False)
+            mm("ID " + hb, "pH", 256, T.pH[:, 0:256], mat("ID"), T.HB[:, b0:b0 + 256], False, k == 15)
         scan("D0 pH", "HUL", 256, T.HUL[:], T.D0[:], T.pH[:, 0:256], -8192.0, Op.min, Op.max)
         tt("FR recvD%d" % t, "FS", 32, lst("FS"), T["DR%d" % t][:], lst("FR"), Op.add)
-        tt("HUL FS", "FR FR0 FR1", 32, lst("FR"), T.HUL[:, 15::16], lst("FS"), Op.is_lt)
+        tt("HUL FS", "FR", 32, lst("FR"), T.HUL[:, 15::16], lst("FS"), Op.is_lt)
         tt("VC VN", "S5", 32, lst("S5"), lst("VC"), lst("VN"), Op.subtract)
         tt("S5 FR", "S6", 32, lst("S6"), lst("S5"), lst("FR"), Op.mult)
         tt("S6 VN", "VC", 32, lst("VC"), lst("S6"), lst("VN"), Op.add)
@@ -293,61 +304,51 @@ def rank_program(g, core, T, topo):
     def keep():
         ts("FR", "THR", 16, lst("THR"), lst("FR"), 1000.0, Op.mult, 9.0, Op.add)
         base()
-        for h in range(2):
-            spread("NF", T.NF, "FR", h)
-        ts("NF0 NF1", "FO", 128, T.FO[:], T.NF[:], -1.0, Op.mult, float(D), Op.add)
-        tt("TR NF0 NF1", "P1", 512, T.P1[:], T.TR[:], T.NF[:], Op.max)
-
-    def wipe(Q):
-        for j in range(0, 8448, 264):
-            op("G", "", "%s%d" % (Q, j // 1056 * 1058), 0.13 + 528 * CYC, lambda e, j=j: e.iota(T[Q][:, j:j + 264], [[0, 264]], 0, 0, allow_small_or_imprecise_dtypes=True))
+        spread("NF", T.NF, "FR")
+        ts("NF", "FO", 128, T.FO[:], T.NF[:], -1.0, Op.mult, float(D), Op.add)
+        tt("TR NF", "P1", 512, T.P1[:], T.TR[:], T.NF[:], Op.max)
 
     cp("V0", "VN", 16, lst("VN"), T.V0[:])
     cp("V0", "VC", 16, lst("VC"), T.V0[:])
-    for h in range(2):
-        rowsum(h, T.SD[:, hs(h)], "SD")
-        squares(h, "SZ%d" % h)
+    rowsum(T.SD, "SD", "SD")
+    squares("SZ")
     base()
 
     for t in range(TS):
         last = t == TS - 1
         Q = "QA" if t % 2 == 0 else "QB"
         zf = "ZF%d" % t
-        vk(0)
-        vk(1)
+        vk()
         places()
         for b in range(4):
-            for h in range(2):
-                step(t, b, h)
-        mm("ID NM", "pH", 256, T.pH[:, 256:512], mat("ID"), T.NM[:], True, False)
-        for h in range(2):
-            halts(t, h)
-            shadows(h)
+            step(t, b)
+        mm("ID NK", "pH", 256, T.pH[:, 256:512], mat("ID"), T.NK[:], True, False)
+        halts(t)
+        shadows()
         if not last:
             send(t, "Z", T["ZP%d" % t][:], T[zf][:], zf + ".0 " + zf + ".1")
         scan("D0 pH", "DUL", 256, T.DUL[:], T.D0[:], T.pH[:, 256:512], -8192.0, Op.min, Op.max)
-        tt("DUL GO0 GO1", "OK", 32, lst("OK"), T.DUL[:, 15::16], lst("GO"), Op.is_lt)
-        tt("OK VD", "L1", 32, lst("L1"), lst("VD"), lst("OK"), Op.mult)
-        tt("L1 DM", "L2", 32, lst("L2"), lst("L1"), T.DM[:], Op.add)
+        tt("DUL VF", "L1", 32, lst("L1"), T.DUL[:, 15::16], lst("VF"), Op.max)
+        tt("L1 DM", "L2", 32, lst("L2"), lst("L1"), T.DM[:], Op.min)
         lq = "LQ%d" % t
         cp("L2", lq, 16, T[lq][:], lst("L2"))
         send(t, "L", T["RL%d" % t][:], T[lq][:], lq)
-        for h in range(2):
-            spread("NG", T.NG, "GO", h)
-            tn = " ".join("TN%d.%d" % (h, b) for b in range(4))
-            tt("%s NG%d" % (tn, h), "M1%d" % h, 256, T.M1[:, hs(h)], T.TN[:, hs(h)], T.NG[:, hs(h)], Op.max)
-            if t == 0:
-                cp("M1%d" % h, "OM%d" % h, 128, T.OM[:, hs(h)], T.M1[:, hs(h)])
-            else:
-                tt("M1%d P1" % h, "M2%d" % h, 256, T.M2[:, hs(h)], T.M1[:, hs(h)], T.P1[:, hs(h)], Op.min)
-                cp("M2%d" % h, "OM%d" % h, 128, T.OM[:, hs(h)], T.M2[:, hs(h)])
+        if t < 3:
+            wipe("QA" if t == 1 else "QB", 0, 16, lq)
+        tn = "TN0 TN1 TN2 TN3"
+        spread("NG", T.NG, "GO")
+        tt(tn + " NG", "M1", 512, T.M1[:], T.TN[:], T.NG[:], Op.max)
+        if t == 0:
+            cp("M1", "OM", 256, T.OM[:], T.M1[:])
+        else:
+            tt("M1 P1", "M2", 512, T.M2[:], T.M1[:], T.P1[:], Op.min)
+            cp("M2", "OM", 256, T.OM[:], T.M2[:])
         rl = T["RL%d" % t]
         rk = "recvL%d" % t
         cp("%s CO %s" % (rk, tabs[Q]), tabs[Q], puts(256), T[Q][:, 0:8448].indirect(rl[:]), T.CO[:])
         cp(rk, "LF", 16, lst("LF"), rl[:])
         ts("LF", "IW", 16, lst("IW"), lst("LF"), float(W), Op.is_lt)
-        tt("LF DM", "LD", 32, lst("LD"), lst("LF"), T.DM[:], Op.subtract)
-        tn = " ".join("TN%d.%d" % (h, b) for b in range(4) for h in range(2))
+        ts("LF", "LD", 16, lst("LD"), lst("LF"), 1.0 / 16384, Op.mult)
         if t == 0:
             cp(tn, "TR", 256, T.TR[:], T.TN[:])
         else:
@@ -355,15 +356,15 @@ def rank_program(g, core, T, topo):
             tt("P1 P2", "TR", 512, T.TR[:], T.P2[:], T.P1[:], Op.min)
             cp("OD ZB " + tabs["HT"], tabs["HT"], puts(256), T.HT[:, 0:8448].indirect(T.OD[:]), T.ZB[:, 0:256])
         if last:
-            for h in range(2):
-                dma("Y", "dz", 32, T.YT[:, :, 8 * h:8 * h + 8], T.TR[:, hs(h)], "TR", "YT%d" % h)
-            dma("Y", "dy", 32, T.yt[:], T.YT[:], "YT0 YT1", "yt")
+            dma("Y", "dy", 32, T.yt[:], T.TR[:], "TR", "yt")
 
         def turn(k):
             b0, pt, a0 = 512 * k, "pT%d" % (k % 2), 512 * (k % 4)
             for j in range(4):
-                op("P", "ID GB%d%s" % (k, "aabb"[j]), pt, 128 * CYC, lambda e, j=j: e.transpose(T[pt][:, 128 * j:128 * j + 128], T.GB[:, b0 + 128 * j:b0 + 128 * j + 128], mat("ID")))
-            ts("%s WH%d0 WH%d1" % (pt, k // 4, k // 4), "LA%d" % (k % 4), 256, T.LA[:, a0:a0 + 512], T[pt][:, 0:512], T.WH[:, k // 4:k // 4 + 1], Op.mult)
+                op("P", "ID GB%d%s" % (k, "aabb"[j]), pt, 128 * CYC, lambda e, j=j: e.transpose(T[pt][:, POS[j]:POS[j] + 128], T.GB[:, b0 + 128 * j:b0 + 128 * j + 128], mat("ID")))
+            for h in range(2):
+                a1 = 256 * h
+                ts("%s WH%d0 WH%d1" % (pt, h, h), "LA%d" % (k % 4), 128, T.LA[:, a0 + a1:a0 + a1 + 256], T[pt][:, a1:a1 + 256], T.WH[:, h:h + 1], Op.mult)
             ts(pt, "LB%d" % (k % 4), 256, T.LB[:, a0:a0 + 512], T[pt][:, 0:512], -1.0, Op.add, 0.0, Op.max)
 
         def cells(k):
@@ -371,7 +372,7 @@ def rank_program(g, core, T, topo):
                 a0 = 512 * (k % 4) + 128 * j
                 mm("LA%d LB%d" % (k % 4, k % 4), "pC", 128, T.pC[:, 128:256], T.LA[:, a0:a0 + 128], T.LB[:, a0:a0 + 128], k == 0 and j == 0, k == 7 and j == 3)
         for k in range(8):
-            key = "%s OM%d" % (tabs[Q], k // 4)
+            key = "%s OM" % tabs[Q]
             if k == 0:
                 cp(key, "GB0a", looks(256), T.GB[:, 0:256], T[Q][:].indirect(T.OM[:, 0:16]))
                 act(key, "GB0b", looks(256), T.GB[:, 256:512], T[Q][:].indirect(T.OM[:, 16:32]), AF.Copy)
@@ -388,16 +389,18 @@ def rank_program(g, core, T, topo):
         tt("MF IW", do, 32, T[do][:], T.MF[:], lst("IW"), Op.is_lt)
         mm("ON " + do, "pC", 16, T.pC[:, 0:16], mat("ON"), T[do][:], True, True)
         send(t, "D", T["DR%d" % t][:], T[do][:], do)
-        tt("LD " + do, "E1", 32, lst("E1"), lst("LD"), T[do][:], Op.mult)
-        tt("E1 DM", "E2", 32, lst("E2"), lst("E1"), T.DM[:], Op.add)
-        cp("E2", "OD", 16, T.OD[:], lst("E2"))
+        tt("LD MF", "E1", 32, lst("E1"), T.MF[:], lst("LD"), Op.max)
+        tt("E1 DS", "E2", 32, lst("E2"), lst("E1"), lst("DS"), Op.min)
+        ts("E2", "OD", 16, T.OD[:], lst("E2"), 16384.0, Op.mult)
         op("V", "pC", "AA", vc(16), lambda e: e.tensor_reduce(T.AA[:], T.pC[:, 0:16], AxisListType.X, Op.add))
         if not last:
             cp("OD recvZ%d" % t, XK, puts(256), T.X[:].indirect(T.OD[:]), T["ZP%d" % t][:])
         ts("BA AA", "S7", 16, lst("S7"), lst("BA"), T.AA[:], Op.add)
         ts("S7", "VN", 16, lst("VN"), lst("S7"), W - 1, Op.bitwise_and)
-        if t < 2:
-            wipe(Q)
+        if t == 0:
+            wipe("QB", 16, 40, "DO0")
+        if 0 < t < 3:
+            wipe("QA" if t == 1 else "QB", 16, 40, do)
         hits(t, (1, 3, 5, 7, 9, 11, 13, 15) if last else HITS_ON_VECTOR)
         if not last:
             keep()
@@ -429,7 +432,7 @@ def rank_program(g, core, T, topo):
                 if k in last_w:
                     after(last_w[k], WAKE)
                 for j in readers.get(k, []):
-                    after(j, WAKE if ops[j]["q"] != o["q"] else 0.0)
+                    after(j, WAKE)
         for k in o["r"] + o["w"]:
             if k[0] == "p":
                 banks.setdefault(k, {})[o["q"]] = i
@@ -536,7 +539,7 @@ def rank_program(g, core, T, topo):
                 toks.append(wr[k])
         for k in o["w"]:
             if k[0] != "p":
-                toks += [tok for q2, tok in rd.get(k, {}).items() if q2 != q]
+                toks += rd.get(k, {}).values()
         best = {}
         for tok in toks:
             if tok[0] not in best or best[tok[0]][1] < tok[1]:

@@ -10,6 +10,7 @@ CM = "ID NI N5 BO TG ON BK TK".split()
 SCRATCH = {
     "X": ("sbuf", [128, 8448], "bfloat16"),
     "QA": ("sbuf", [128, 8464], "bfloat16"), "QB": ("sbuf", [128, 8464], "bfloat16"), "HT": ("sbuf", [128, 8464], "bfloat16"),
+    "OW": ("sbuf", [128, 1024], "bfloat16"),
     "IO": ("sbuf", [128, 8192], "float32"),
     "SD": ("sbuf", [128, 256], "bfloat16"), "V0": ("sbuf", [128, 16], "int32"), "TI": ("sbuf", [128, 4], "int32"), "TF": ("sbuf", [128, 4], "float32"),
     "PI": ("sbuf", [128, 4], "int32"), "PF": ("sbuf", [128, 4], "float32"),
@@ -19,7 +20,7 @@ SCRATCH = {
     "KA": ("sbuf", [128, 256], "float32"), "KC": ("sbuf", [128, 256], "float32"), "NK": ("sbuf", [128, 256], "bfloat16"),
     "NM": ("sbuf", [128, 256], "bfloat16"), "CO": ("sbuf", [128, 256], "bfloat16"), "D0": ("sbuf", [128, 256], "float32"),
     "TH": ("sbuf", [128, 128], "float32"), "WH": ("sbuf", [128, 2], "float32"), "DM": ("sbuf", [128, 16], "float32"),
-    "OB": ("sbuf", [128, 256], "bfloat16"), "ZB": ("sbuf", [128, 264], "bfloat16"),
+    "OB": ("sbuf", [128, 256], "bfloat16"), "ZB": ("sbuf", [128, 529], "bfloat16"),
     "TN": ("sbuf", [128, 256], "int32"), "TR": ("sbuf", [128, 256], "float32"), "P1": ("sbuf", [128, 256], "float32"),
     "P2": ("sbuf", [128, 256], "float32"), "M1": ("sbuf", [128, 256], "float32"), "M2": ("sbuf", [128, 256], "float32"),
     "OM": ("sbuf", [128, 256], "uint16"), "NG": ("sbuf", [128, 256], "bfloat16"), "NF": ("sbuf", [128, 256], "bfloat16"), "FO": ("sbuf", [128, 256], "bfloat16"),
@@ -29,7 +30,7 @@ SCRATCH = {
     "MC": ("sbuf", [128, 128], "bfloat16"), "MD": ("sbuf", [128, 64], "bfloat16"), "ME": ("sbuf", [128, 32], "bfloat16"), "MF": ("sbuf", [128, 16], "bfloat16"),
     "AA": ("sbuf", [128, 1], "float32"), "YT": ("sbuf", [128, 16, 16], "float32"), "YS": ("sbuf", [128, 32], "float32"),
     "GB": ("sbuf", [128, 4096], "bfloat16"), "HB": ("sbuf", [128, 2048], "bfloat16"), "LA": ("sbuf", [128, 2048], "bfloat16"), "LB": ("sbuf", [128, 2048], "bfloat16"),
-    "pU": ("psum", [128, 512], "float32"), "pD0": ("psum", [128, 512], "float32"), "pD1": ("psum", [128, 512], "float32"),
+    "pU0": ("psum", [128, 512], "float32"), "pU1": ("psum", [128, 512], "float32"), "pD0": ("psum", [128, 512], "float32"), "pD1": ("psum", [128, 512], "float32"),
     "pT0": ("psum", [128, 1024], "bfloat16"), "pT1": ("psum", [128, 1024], "bfloat16"), "pC": ("psum", [128, 512], "float32"), "pH": ("psum", [128, 512], "float32"),
 }
 SCRATCH.update({"Z": ("sbuf", [128, 256], "bfloat16"), "Y": ("sbuf", [128, 1024], "bfloat16"), "F": ("sbuf", [128, 256], "bfloat16"),
@@ -40,11 +41,13 @@ for _t in range(TS):
                     "RL%d" % _t: ("sbuf", [128, 16], "uint16"), "DO%d" % _t: ("sbuf", [128, 16], "bfloat16"), "DR%d" % _t: ("sbuf", [128, 16], "bfloat16")})
 SEMAPHORES = ["cV", "cS", "cP", "cG", "dx", "dv", "ds", "dt", "dy", "dz", "loc"] + ["r%s%d" % (k, t) for k in "LZD" for t in range(TS)]
 CYC, WAKE, SFIX, LOOK, PUT, REMOTE = 0.00083, 0.15, 0.15, 1.3, 3.0, 3.0
-MARGIN = 3
+MARGIN, AHEAD = 2, 0.0
+STIR, SEED = 0.0, 0
+ORDER = []
 SFIRST = (1,)
 GAP = {"S": 0.3, "V": 0.9}
 POS = (0, 256, 128, 384)
-HITS_ON_VECTOR = (2, 5, 8, 11, 14)
+HITS_ON_VECTOR = (4, 9, 14)
 
 
 def rank_program(g, core, T, topo):
@@ -53,10 +56,11 @@ def rank_program(g, core, T, topo):
         return
     eng = {"V": g.vector, "S": g.scalar, "P": g.tensor, "G": g, "Y": g.sync}
     ops = []
+    boost = [0.0]
     chain = [None]
 
     def op(q, reads, writes, cost, f, kind="c", sem=None, n=0, lat=0.0):
-        ops.append({"chain": chain[0], "q": q, "r": reads.split(), "w": writes.split(), "cost": cost, "f": f, "kind": kind, "sem": sem, "n": n, "lat": lat})
+        ops.append({"chain": chain[0], "first": boost[0], "q": q, "r": reads.split(), "w": writes.split(), "cost": cost, "f": f, "kind": kind, "sem": sem, "n": n, "lat": lat})
 
     def dma(q, sem, total, out, in_, reads, writes):
         op(q, reads, writes, 0.1, lambda e: e.dma_start(out, in_).then_inc(T.sem[sem], 16), "d", sem, total, 7.0 if sem == "dx" else 2.5)
@@ -160,7 +164,9 @@ def rank_program(g, core, T, topo):
     ts("DMI PF", "DM", 16, T.DM[:], T.DM[:], pi, Op.add)
     ts("DM", "DS", 16, lst("DS"), T.DM[:], 1.0 / 16384, Op.mult)
     fill("OB", 128, T.OB[:], 1.0)
-    fill("ZB", 128, T.ZB[:], 0.0)
+    for t in range(TS):
+        fill("OW%d" % t, 128, T.OW[:, 256 * t:256 * t + 256], 32.0 ** (t + 1 - TS))
+    fill("ZB", 265, T.ZB[:], 0.0)
     fill("ON", 64, mat("ON"), 1.0)
     fill("SC0", 1, T.SC[:, 0:1], 0.0)
     fill("THR", 16, lst("THR"), 9.0)
@@ -188,29 +194,33 @@ def rank_program(g, core, T, topo):
     for j in range(0, 8464, 1058):
         fill("QA" + str(j), 529, T.QA[:, j:j + 1058], 0.0)
         for i in range(j, j + 1058, 264):
-            n = min(264, j + 1058 - i)
-            act("ZB", "HT" + str(j), n, T.HT[:, i:i + n], T.ZB[:, 0:n], AF.Copy)
-            pieces.append((str(j), i, n))
+            pieces.append((str(j), i, min(264, j + 1058 - i)))
+
+    for key, i, n in pieces:
+        act("ZB", "HT" + key, n, T.HT[:, i:i + n], T.ZB[:, 0:n], AF.Copy)
 
     def wipe(Q, a, b, behind):
         for key, i, n in pieces[a:b]:
             op("G", behind, Q + key, 0.13 + 2 * n * CYC, lambda e, i=i, n=n: e.iota(T[Q][:, i:i + n], [[0, n]], 0, 0, allow_small_or_imprecise_dtypes=True))
-    tabs = {buf: " ".join(buf + str(j) for j in range(0, 8464, 1058)) for buf in ("QA", "HT", "QB")}
+    tabs = {buf: " ".join(buf + str(j) for j in range(0, 8464, 1058)) for buf in ("QA", "QB", "HT")}
 
     def hs(h):
         return slice(128 * h, 128 * h + 128)
 
     def rowsum(src, key0, key1):
-        mm("ID NM", "pU", 256, T.pU[:, 0:256], mat("ID"), T.NM[:], True, False)
-        mm("BO " + key0, "pU", 128, T.pU[:, 0:128], mat("BO"), src[:, 0:128], False, False)
-        mm("BO " + key1, "pU", 128, T.pU[:, 128:256], mat("BO"), src[:, 128:256], False, True)
-        scan("D0 pU", "UL", 256, T.UL[:], T.D0[:], T.pU[:, 0:256], -8192.0, Op.min, Op.max)
+        for h, key in ((0, key0), (1, key1)):
+            u = "pU%d" % h
+            mm("ID NM", u, 128, T[u][:, 0:128], mat("ID"), T.NM[:, 0:128], True, False)
+            mm("BO " + key, u, 128, T[u][:, 0:128], mat("BO"), src[:, hs(h)], False, True)
+            scan("D0 " + u, "UL%d" % h, 128, T.UL[:, hs(h)], T.D0[:, 0:128], T[u][:, 0:128], -8192.0, Op.min, Op.max)
+
+    SQK = "SQ.0 SQ.1 SQ.2"
 
     def squares(dst):
         for m in range(2):
-            act("UL", "%s.%d" % (dst, m), 16, T[dst][:, 16 * m:16 * m + 16], T.UL[:, 15::16], AF.Square, bias=2.0 * KAPPA[m], scale=0.25)
+            act("UL0 UL1", "%s.%d" % (dst, m), 16, T[dst][:, 16 * m:16 * m + 16], T.UL[:, 15::16], AF.Square, bias=2.0 * KAPPA[m], scale=0.25)
         for m in (2, 3):
-            ts("UL", "XQ%d" % m, 16, T.XQ[:, 16 * m - 32:16 * m - 16], T.UL[:, 15::16], 0.25, Op.mult, 2.0 * KAPPA[m], Op.add)
+            ts("UL0 UL1", "XQ%d" % m, 16, T.XQ[:, 16 * m - 32:16 * m - 16], T.UL[:, 15::16], 0.25, Op.mult, 2.0 * KAPPA[m], Op.add)
         tt("XQ2 XQ3", "%s.2" % dst, 64, T[dst][:, 32:64], T.XQ[:], T.XQ[:], Op.mult)
 
     def vk():
@@ -224,12 +234,16 @@ def rank_program(g, core, T, topo):
         for h in range(2):
             src, zk = (T.SD[:, hs(h)], "SD") if b == 0 else (T.Z[:, hs(h)], "Z%d" % h)
             mm("NI " + zk, "pD%d" % h, 128, T["pD%d" % h][:, 0:128], mat("NI"), src, True, False)
-        sq = "SQ" if b else "SZ"
         tn = "TN%d" % b
-        tt("%s.0 %s.1 %s.2 VK0 VK1 VK2 VK3" % (sq, sq, sq), "XI", 128, T.XI[:], T[sq][:], T.VK[:], Op.add)
-        ts("XI", tn, 64, T.TN[:, 64 * b:64 * b + 64], T.XI[:], W - 1, Op.bitwise_and)
+        if b:
+            tt(SQK + " VK0 VK1 VK2 VK3", "XI0 XI1 XI2 XI3", 128, T.XI[:], T.SQ[:], T.VK[:], Op.add)
+        else:
+            for m in range(4):
+                tt("SY%d VN" % m, "XI%d" % m, 32, T.XI[:, 16 * m:16 * m + 16], T.SZ[:, 16 * m:16 * m + 16], lst("VN"), Op.add)
+        ts("XI0 XI1 XI2 XI3", tn, 64, T.TN[:, 64 * b:64 * b + 64], T.XI[:], W - 1, Op.bitwise_and)
         cp(tn, "OF", 64, T.OF[:], T.TN[:, 64 * b:64 * b + 64])
         for h in range(2):
+            boost[0] = AHEAD * (1 - h)
             look = [T.X[:, 0:W].indirect(T.OF[:, 16 * m + 8 * h:16 * m + 8 * h + 8]) for m in range(4)]
             y, d = "Y%d." % h, "pD%d" % h
             ys = [T.Y[:, 256 * m + 128 * h:256 * m + 128 * h + 128] for m in range(4)]
@@ -244,6 +258,7 @@ def rank_program(g, core, T, topo):
                 act(d, "Z%d" % h, 128, T.Z[:, hs(h)], T[d][:, 0:128], AF.Abs)
             else:
                 act(d, "ZF%d.%d" % (t, h), 128, T["ZF%d" % t][:, hs(h)], T[d][:, 0:128], AF.Abs)
+        boost[0] = 0.0
 
     def spread(key, out, src):
         act(src, key, 16, out[:, 0:16], lst(src), AF.Identity, bias=float(D), scale=-float(D))
@@ -254,7 +269,7 @@ def rank_program(g, core, T, topo):
         for h in range(2):
             ts("ZF%d.%d TF" % (t, h), "F%d" % h, 64, T.F[:, hs(h)], T["ZF%d" % t][:, hs(h)], T.TF[:, t:t + 1], Op.is_ge)
         rowsum(T.F, "F0", "F1")
-        tt("UL THR", "HA", 32, T.HA[:], T.UL[:, 15::16], lst("THR"), Op.is_ge)
+        tt("UL0 UL1 THR", "HA", 32, T.HA[:], T.UL[:, 15::16], lst("THR"), Op.is_ge)
         mm("TG HA", "pC", 16, T.pC[:, 0:16], mat("TG"), T.HA[:], True, False)
         mm("N5 HA", "pC", 16, T.pC[:, 0:16], mat("N5"), T.HA[:], False, False)
         scan("OB HA", "SC1", 16, T.SC[:, 1:17], T.OB[:, 0:16], T.HA[:], 0.0, Op.mult, Op.add)
@@ -264,9 +279,9 @@ def rank_program(g, core, T, topo):
     def shadows():
         for c in range(16):
             ts("DV VF GO", "EB%d" % c, (L - 16 * c) // 2, T.EB[:, c, 0:L - 16 * c], T.DV[:, 16 * c:L], part("VF", c, c + 1), Op.is_equal, part("GO", c, c + 1), Op.mult)
-            mm("TK EB%d" % c, "pH", 16, T.pH[:, 256 + 16 * c:272 + 16 * c], mat("TK"), T.EB[:, c, 0:16], False, c == 15)
             if c < 15:
                 mm("BK EB%d" % c, "pH", L - 16 - 16 * c, T.pH[:, 272 + 16 * c:512], mat("BK"), T.EB[:, c, 16:L - 16 * c], False, False)
+        mm("TK " + " ".join("EB%d" % c for c in range(16)), "pH", 256, T.pH[:, 256:512], mat("TK"), T.EB[:, :, 0:16], False, True)
 
     def places():
         cp("VN", "OV", 16, T.OV[:], lst("VN"))
@@ -281,7 +296,8 @@ def rank_program(g, core, T, topo):
         tt("S3 S4", "BA", 32, lst("BA"), lst("S4"), lst("S3"), Op.add)
 
     def hits(t, onv):
-        cp("OD OB " + tabs["HT"], tabs["HT"], puts(256), T.HT[:, 0:8448].indirect(T.OD[:]), T.OB[:])
+        mark = 32.0 ** (t + 1 - TS)
+        cp("OD OW%d " % t + tabs["HT"], tabs["HT"], puts(256), T.HT[:, 0:8448].indirect(T.OD[:]), T.OW[:, 256 * t:256 * t + 256])
         for k in range(16):
             hb, b0 = "HB%d" % (k % 8), 256 * (k % 8)
             src, key = T.HT[:].indirect(T.OM[:, 16 * k:16 * k + 16]), "%s OM" % tabs["HT"]
@@ -296,10 +312,13 @@ def rank_program(g, core, T, topo):
             mm("ID " + hb, "pH", 256, T.pH[:, 0:256], mat("ID"), T.HB[:, b0:b0 + 256], False, k == 15)
         scan("D0 pH", "HUL", 256, T.HUL[:], T.D0[:], T.pH[:, 0:256], -8192.0, Op.min, Op.max)
         tt("FR recvD%d" % t, "FS", 32, lst("FS"), T["DR%d" % t][:], lst("FR"), Op.add)
-        tt("HUL FS", "FR", 32, lst("FR"), T.HUL[:, 15::16], lst("FS"), Op.is_lt)
+        if mark != 1.0:
+            ts("FS", "FS", 16, lst("FS"), lst("FS"), mark, Op.mult)
+        fr, v = (T.YS[:, 16:32], T.YS[:, 0:16]) if t == TS - 1 else (lst("FR"), lst("VC"))
         tt("VC VN", "S5", 32, lst("S5"), lst("VC"), lst("VN"), Op.subtract)
-        tt("S5 FR", "S6", 32, lst("S6"), lst("S5"), lst("FR"), Op.mult)
-        tt("S6 VN", "VC", 32, lst("VC"), lst("S6"), lst("VN"), Op.add)
+        tt("HUL FS", "FR", 32, fr, T.HUL[:, 15::16], lst("FS"), Op.is_lt)
+        tt("S5 FR", "S6", 32, lst("S6"), lst("S5"), fr, Op.mult)
+        tt("S6 VN", "VC", 32, v, lst("S6"), lst("VN"), Op.add)
 
     def keep():
         ts("FR", "THR", 16, lst("THR"), lst("FR"), 1000.0, Op.mult, 9.0, Op.add)
@@ -312,6 +331,8 @@ def rank_program(g, core, T, topo):
     cp("V0", "VC", 16, lst("VC"), T.V0[:])
     rowsum(T.SD, "SD", "SD")
     squares("SZ")
+    for m in range(4):
+        ts("SZ.%d" % min(m, 2), "SY%d" % m, 16, T.SZ[:, 16 * m:16 * m + 16], T.SZ[:, 16 * m:16 * m + 16], -4.0 * KAPPA[m] ** 2 - 0.25, Op.add)
     base()
 
     for t in range(TS):
@@ -354,7 +375,6 @@ def rank_program(g, core, T, topo):
         else:
             tt(tn + " FO", "P2", 512, T.P2[:], T.TN[:], T.FO[:], Op.max)
             tt("P1 P2", "TR", 512, T.TR[:], T.P2[:], T.P1[:], Op.min)
-            cp("OD ZB " + tabs["HT"], tabs["HT"], puts(256), T.HT[:, 0:8448].indirect(T.OD[:]), T.ZB[:, 0:256])
         if last:
             dma("Y", "dy", 32, T.yt[:], T.TR[:], "TR", "yt")
 
@@ -404,9 +424,7 @@ def rank_program(g, core, T, topo):
         hits(t, (1, 3, 5, 7, 9, 11, 13, 15) if last else HITS_ON_VECTOR)
         if not last:
             keep()
-    cp("VC", "YS", 16, T.YS[:, 0:16], lst("VC"))
-    cp("FR", "YS", 16, T.YS[:, 16:32], lst("FR"))
-    dma("Y", "dy", 32, T.ys[:], T.YS[:], "YS", "ys")
+    dma("Y", "dy", 32, T.ys[:], T.YS[:], "FR VC", "ys")
 
     N = len(ops)
     preds = [dict() for _ in ops]
@@ -453,7 +471,9 @@ def rank_program(g, core, T, topo):
         for j, wake in succs[i]:
             gap = GAP[ops[i]["chain"]] if ops[i]["chain"] and ops[i]["chain"] == ops[j]["chain"] else 0.0
             best = max(best, wake + ops[i]["lat"] + gap + prio[j])
-        prio[i] = best + ops[i]["cost"]
+        prio[i] = best + ops[i]["cost"] + ops[i]["first"]
+        if STIR:
+            prio[i] += STIR * ((i * 7919 + SEED * 104729) * 2654435761 % 4294967296) / 4294967296
     left = [len(preds[i]) for i in range(N)]
     ready = [0.0] * N
     free = {q: 0.0 for q in eng}
@@ -479,6 +499,7 @@ def rank_program(g, core, T, topo):
             memo[i] = best
         return memo[i]
 
+    order += ORDER
     while len(order) < N:
         pick = None
         for q in "VSPGY":
@@ -515,6 +536,9 @@ def rank_program(g, core, T, topo):
             left[j] -= 1
             if left[j] == 0:
                 avail[ops[j]["q"]].append(j)
+
+    if not ORDER:
+        ORDER.extend(order)
 
     count = {q: 0 for q in eng}
     clock = {q: {} for q in eng}

from concourse.mybir import AluOpType as Op, AxisListType, ActivationFunctionType as AF

W, L, D = 8192, 256, 8448
KAPPA = (3, 29, 71, 113)
TS, CAP = 4, 128
FL = "GO THR DS L1 L2 LF IW LD E1 E2 FR FS VF BA S4 S5 S6".split()
IL = "VN VC S1 S2 S3 S7".split()
CM = "ID NI N5 BO TG ON BK TK".split()

SCRATCH = {
    "X": ("sbuf", [128, 8448], "bfloat16"),
    "QA": ("sbuf", [128, 8464], "bfloat16"), "QB": ("sbuf", [128, 8464], "bfloat16"), "HT": ("sbuf", [128, 8464], "bfloat16"),
    "OW": ("sbuf", [128, 1024], "bfloat16"),
    "IO": ("sbuf", [128, 8192], "float32"),
    "SD": ("sbuf", [128, 256], "bfloat16"), "V0": ("sbuf", [128, 16], "int32"), "TI": ("sbuf", [128, 4], "int32"), "TF": ("sbuf", [128, 4], "float32"),
    "PI": ("sbuf", [128, 4], "int32"), "PF": ("sbuf", [128, 4], "float32"),
    "RM": ("sbuf", [128, 256], "float32"), "RD": ("sbuf", [128, 256], "float32"), "RP": ("sbuf", [128, 128], "float32"), "RG": ("sbuf", [128, 128], "float32"),
    "K1": ("sbuf", [128, 256], "float32"), "K2": ("sbuf", [128, 256], "float32"), "K3": ("sbuf", [128, 256], "float32"), "K4": ("sbuf", [128, 256], "float32"),
    "CM": ("sbuf", [128, 128 * len(CM)], "bfloat16"), "FL": ("sbuf", [128, 16 * len(FL)], "float32"), "IL": ("sbuf", [128, 16 * len(IL)], "int32"),
    "KA": ("sbuf", [128, 256], "float32"), "KC": ("sbuf", [128, 256], "float32"), "NK": ("sbuf", [128, 256], "bfloat16"),
    "NM": ("sbuf", [128, 256], "bfloat16"), "CO": ("sbuf", [128, 256], "bfloat16"), "D0": ("sbuf", [128, 256], "float32"),
    "TH": ("sbuf", [128, 128], "float32"), "WH": ("sbuf", [128, 2], "float32"), "DM": ("sbuf", [128, 16], "float32"),
    "OB": ("sbuf", [128, 256], "bfloat16"), "ZB": ("sbuf", [128, 529], "bfloat16"),
    "TN": ("sbuf", [128, 256], "int32"), "TR": ("sbuf", [128, 256], "float32"), "P1": ("sbuf", [128, 256], "float32"),
    "P2": ("sbuf", [128, 256], "float32"), "M1": ("sbuf", [128, 256], "float32"), "M2": ("sbuf", [128, 256], "float32"),
    "OM": ("sbuf", [128, 256], "uint16"), "NG": ("sbuf", [128, 256], "bfloat16"), "NF": ("sbuf", [128, 256], "bfloat16"), "FO": ("sbuf", [128, 256], "bfloat16"),
    "OV": ("sbuf", [128, 16], "uint16"), "DV": ("sbuf", [128, 256], "uint16"), "OD": ("sbuf", [128, 16], "uint16"),
    "HA": ("sbuf", [128, 16], "bfloat16"), "SC": ("sbuf", [128, 18], "bfloat16"),
    "EB": ("sbuf", [128, 16, 256], "bfloat16"), "DUL": ("sbuf", [128, 256], "float32"), "HUL": ("sbuf", [128, 256], "float32"),
    "MC": ("sbuf", [128, 128], "bfloat16"), "MD": ("sbuf", [128, 64], "bfloat16"), "ME": ("sbuf", [128, 32], "bfloat16"), "MF": ("sbuf", [128, 16], "bfloat16"),
    "AA": ("sbuf", [128, 1], "float32"), "YT": ("sbuf", [128, 16, 16], "float32"), "YS": ("sbuf", [128, 32], "float32"),
    "GB": ("sbuf", [128, 4096], "bfloat16"), "HB": ("sbuf", [128, 2048], "bfloat16"), "LA": ("sbuf", [128, 2048], "bfloat16"), "LB": ("sbuf", [128, 2048], "bfloat16"),
    "pU0": ("psum", [128, 512], "float32"), "pU1": ("psum", [128, 512], "float32"), "pD0": ("psum", [128, 512], "float32"), "pD1": ("psum", [128, 512], "float32"),
    "pT0": ("psum", [128, 1024], "bfloat16"), "pT1": ("psum", [128, 1024], "bfloat16"), "pC": ("psum", [128, 512], "float32"), "pH": ("psum", [128, 512], "float32"),
}
SCRATCH.update({"Z": ("sbuf", [128, 256], "bfloat16"), "Y": ("sbuf", [128, 1024], "bfloat16"), "F": ("sbuf", [128, 256], "bfloat16"),
                "UL": ("sbuf", [128, 256], "float32"), "SQ": ("sbuf", [128, 64], "float32"), "SZ": ("sbuf", [128, 64], "float32"), "XQ": ("sbuf", [128, 32], "float32"),
                "XI": ("sbuf", [128, 64], "int32"), "OF": ("sbuf", [128, 64], "uint16"), "VK": ("sbuf", [128, 64], "float32")})
for _t in range(TS):
    SCRATCH.update({"ZF%d" % _t: ("sbuf", [128, 256], "bfloat16"), "ZP%d" % _t: ("sbuf", [128, 256], "bfloat16"), "LQ%d" % _t: ("sbuf", [128, 16], "uint16"),
                    "RL%d" % _t: ("sbuf", [128, 16], "uint16"), "DO%d" % _t: ("sbuf", [128, 16], "bfloat16"), "DR%d" % _t: ("sbuf", [128, 16], "bfloat16")})
SEMAPHORES = ["cV", "cS", "cP", "cG", "dx", "dv", "ds", "dt", "dy", "dz", "loc"] + ["r%s%d" % (k, t) for k in "LZD" for t in range(TS)]
CYC, WAKE, SFIX, LOOK, PUT, REMOTE = 0.00083, 0.15, 0.15, 1.3, 3.0, 3.0
MARGIN, AHEAD = 2, 0.0
STIR, SEED = 0.0, 0
ORDER = []
SFIRST = (1,)
GAP = {"S": 0.3, "V": 0.9}
POS = (0, 256, 128, 384)
HITS_ON_VECTOR = (4, 9, 14)


def rank_program(g, core, T, topo):
    rank = T.rank_of(core)
    if rank is None:
        return
    eng = {"V": g.vector, "S": g.scalar, "P": g.tensor, "G": g, "Y": g.sync}
    ops = []
    boost = [0.0]
    chain = [None]

    def op(q, reads, writes, cost, f, kind="c", sem=None, n=0, lat=0.0):
        ops.append({"chain": chain[0], "first": boost[0], "q": q, "r": reads.split(), "w": writes.split(), "cost": cost, "f": f, "kind": kind, "sem": sem, "n": n, "lat": lat})

    def dma(q, sem, total, out, in_, reads, writes):
        op(q, reads, writes, 0.1, lambda e: e.dma_start(out, in_).then_inc(T.sem[sem], 16), "d", sem, total, 7.0 if sem == "dx" else 2.5)

    def part(k, a, b):
        for group, buf, w in ((FL, "FL", 16), (IL, "IL", 16), (CM, "CM", 128)):
            if k in group:
                o = w * group.index(k)
                return T[buf][:, o + a:o + b]
        return T[k][:, a:b]

    def lst(k):
        return part(k, 0, 16)

    def mat(k):
        return part(k, 0, 128)

    def vc(n):
        return 0.02 + max(n, 64) * CYC

    def ts(reads, writes, n, out, in0, s1, o1, s2=None, o2=None):
        if o2 is None:
            op("V", reads, writes, vc(n), lambda e: e.tensor_scalar(out, in0, s1, None, o1))
        else:
            op("V", reads, writes, vc(n), lambda e: e.tensor_scalar(out, in0, s1, s2, o1, o2))

    def tt(reads, writes, n, out, in0, in1, o):
        op("V", reads, writes, vc(n), lambda e: e.tensor_tensor(out, in0, in1, o))

    def cp(reads, writes, n, out, in_):
        op("V", reads, writes, vc(n), lambda e: e.tensor_copy(out, in_))

    def act(reads, writes, n, out, in_, fn, bias=0.0, scale=1.0):
        op("S", reads, writes, SFIX + n * CYC, lambda e: e.activation(out, in_, fn, bias=bias, scale=scale))

    def mm(reads, writes, n, out, lhsT, rhs, a, z):
        op("P", reads, writes, vc(n), lambda e: e.matmul(out, lhsT, rhs, a, z))

    def scan(reads, writes, n, out, d0, d1, init, o0, o1):
        op("V", reads, writes, vc(n), lambda e: e.tensor_tensor_scan(out, d0, d1, init, o0, o1))

    def fill(key, n, ap, c):
        op("V", "", key, vc(n), lambda e: e.memset(ap, c))

    def iota(key, n, out, pat, base, cm):
        op("G", "", key, 0.13 + 2 * n * CYC, lambda e: e.iota(out, pat, base, cm, allow_small_or_imprecise_dtypes=True))

    def looks(n):
        return LOOK * n + 60

    def puts(n):
        return PUT * n + 60
    sent = [0]

    def send(t, kind, dst, src, keys):
        to = T.cores[rank ^ (1 + t % (len(T.cores) - 1))]
        rid, pid = topo.addr(to)[:2]
        m = topo.mask(core, to)
        n = bin(m).count("1")
        sem = "r%s%d" % (kind, t)
        sent[0] += n
        op("G", keys, "recv%s%d" % (kind, t), 0.3, lambda e: e.remote_dma(dst, src, T.sem[sem], T.sem.loc, pid, rid, m), "r", sem, n, REMOTE)

    XK = "Xa Xb"
    dma("S", "dv", 16, T.V0[:], T.v0[:], "", "V0")
    dma("S", "ds", 16, T.SD[:], T.sd[:], "", "SD")
    dma("S", "dt", 16, T.TI[:], T.th[:], "", "TI")
    dma("Y", "dx", 32, T.X[0:64, 0:W], T.x[0:64, :], "", "Xa")
    dma("Y", "dx", 32, T.X[64:128, 0:W], T.x[64:128, :], "", "Xb")

    iota("PI0", 1, T.PI[:, 0:1], [[0, 1]], 0, 1)
    iota("RM", 256, T.RM[:], [[0, 16], [1, 16]], 0, 0)
    iota("RP", 128, T.RP[:], [[1, 128]], 0, 0)
    iota("RG", 128, T.RG[:], [[1, 8], [0, 16]], 0, 0)
    iota("RD", 256, T.RD[:], [[1, 16], [0, 16]], 0, 0)
    iota("DMI", 16, T.DM[:], [[16, 16]], W, 0)
    for j in range(8):
        iota("IO%d" % j, 512, T.IO[:, 512 * j:512 * j + 512], [[1, 512]], 512 * j, 0)
        act("IO%d" % j, "IO%d" % (j + 8), 512, T.IO[:, 512 * j + 4096:512 * j + 4608], T.IO[:, 512 * j:512 * j + 512], AF.Identity, bias=4096.0)
    IOK = " ".join("IO%d" % j for j in range(16))
    ts("PI0", "PI1", 1, T.PI[:, 1:2], T.PI[:, 0:1], 15, Op.bitwise_and)
    ts("PI0", "PI2", 1, T.PI[:, 2:3], T.PI[:, 0:1], 4, Op.arith_shift_right)
    cp("PI0 PI1 PI2", "PF", 3, T.PF[:, 0:3], T.PI[:, 0:3])
    p, pi, pg = T.PF[:, 0:1], T.PF[:, 1:2], T.PF[:, 2:3]
    ts("RM PF", "NM", 256, T.NM[:], T.RM[:], pi, Op.not_equal, -8192.0, Op.mult)
    ts("RG PF", "BO", 128, mat("BO"), T.RG[:], pg, Op.is_equal)
    ts("RM", "K4", 256, T.K4[:], T.RM[:], 0.0, Op.is_equal, -65536.0, Op.mult)
    ts("K4", "D0", 256, T.D0[:], T.K4[:], 32768.0, Op.add)
    ts("RP PF", "ID", 128, mat("ID"), T.RP[:], p, Op.is_equal)
    ts("RP PF", "NI", 128, mat("NI"), T.RP[:], p, Op.is_equal, -1.0, Op.mult)
    ts("RP PF", "N5", 128, mat("N5"), T.RP[:], p, Op.is_equal, -512.0, Op.mult)
    ts("RM PF", "K1", 256, T.K1[:], T.RM[:], pi, Op.is_equal)
    ts("RM PF", "K2", 128, T.K2[:, 0:128], T.RM[:, 0:128], pi, Op.is_gt)
    tt("K2 BO", "TG", 256, mat("TG"), T.K2[:, 0:128], mat("BO"), Op.mult)
    ts("BO", "BK", 128, mat("BK"), mat("BO"), 32768.0, Op.mult)
    ts("ID", "KA", 128, T.KA[:, 0:128], mat("ID"), -16384.0, Op.mult)
    ts("TG", "KB", 128, T.KA[:, 128:256], mat("TG"), 32768.0, Op.mult)
    tt("KA KB", "TK", 256, mat("TK"), T.KA[:, 0:128], T.KA[:, 128:256], Op.add)
    ts("RM PF", "KC", 256, T.KC[:], T.RM[:], pi, Op.not_equal, -float(2 ** 24 + 2 ** 14), Op.mult)
    ts("KC", "NK", 256, T.NK[:], T.KC[:], 16384.0, Op.add)
    ts("DMI PF", "DM", 16, T.DM[:], T.DM[:], pi, Op.add)
    ts("DM", "DS", 16, lst("DS"), T.DM[:], 1.0 / 16384, Op.mult)
    fill("OB", 128, T.OB[:], 1.0)
    for t in range(TS):
        fill("OW%d" % t, 128, T.OW[:, 256 * t:256 * t + 256], 32.0 ** (t + 1 - TS))
    fill("ZB", 265, T.ZB[:], 0.0)
    fill("ON", 64, mat("ON"), 1.0)
    fill("SC0", 1, T.SC[:, 0:1], 0.0)
    fill("THR", 16, lst("THR"), 9.0)
    fill("FR", 16, lst("FR"), 0.0)
    cp("TI", "TF", 4, T.TF[:], T.TI[:])
    ts("RD PF", "K2", 256, T.K2[:], T.RD[:], pi, Op.is_equal, 2.0, Op.mult)
    tt("K1 K2", "K3", 512, T.K3[:], T.K1[:], T.K2[:], Op.mult)
    ts("K3", "K3", 256, T.K3[:], T.K3[:], 4194304.0, Op.mult)
    tt("K1 K3", "K3", 512, T.K3[:], T.K3[:], T.K1[:], Op.add)
    tt("K2 K3", "CO", 512, T.CO[:], T.K3[:], T.K2[:], Op.add)
    fill("TH0", 16, T.TH[:, 0:4], 0.75 * 2.0 ** 33)
    for k in range(1, 4):
        fill("TH%d" % k, 16, T.TH[:, 4 * k:4 * k + 4], 0.75 * 2.0 ** (11 * (3 - k)))
    cp("TH0 TH1 TH2 TH3", "TH4", 16, T.TH[:, 16:32], T.TH[:, 0:16])
    cp("TH0 TH1 TH2 TH3 TH4", "TH5", 32, T.TH[:, 32:64], T.TH[:, 0:32])
    cp("TH0 TH1 TH2 TH3 TH4 TH5", "TH", 64, T.TH[:, 64:128], T.TH[:, 0:64])
    ts("K1", "K4", 128, T.K4[:, 0:128], T.K1[:, 0:128], 2.0 ** 46, Op.mult, 1.0, Op.max)
    tt("K4 TH TH5", "TH", 256, T.TH[:], T.TH[:], T.K4[:, 0:128], Op.mult)
    ts("BO", "K3", 128, T.K3[:, 0:128], mat("BO"), 0.0, Op.is_equal, 1.0e29, Op.mult)
    tt("K3 TH", "TH", 256, T.TH[:], T.TH[:], T.K3[:, 0:128], Op.max)
    for h in range(2):
        for a in range(2):
            fill("WH%d%d" % (h, a), 1, T.WH[64 * a:64 * a + 64, h:h + 1], 2.0 ** (11 * (3 - 2 * h - a)))
    pieces = []
    for j in range(0, 8464, 1058):
        fill("QA" + str(j), 529, T.QA[:, j:j + 1058], 0.0)
        for i in range(j, j + 1058, 264):
            pieces.append((str(j), i, min(264, j + 1058 - i)))

    for key, i, n in pieces:
        act("ZB", "HT" + key, n, T.HT[:, i:i + n], T.ZB[:, 0:n], AF.Copy)

    def wipe(Q, a, b, behind):
        for key, i, n in pieces[a:b]:
            op("G", behind, Q + key, 0.13 + 2 * n * CYC, lambda e, i=i, n=n: e.iota(T[Q][:, i:i + n], [[0, n]], 0, 0, allow_small_or_imprecise_dtypes=True))
    tabs = {buf: " ".join(buf + str(j) for j in range(0, 8464, 1058)) for buf in ("QA", "QB", "HT")}

    def hs(h):
        return slice(128 * h, 128 * h + 128)

    def rowsum(src, key0, key1):
        for h, key in ((0, key0), (1, key1)):
            u = "pU%d" % h
            mm("ID NM", u, 128, T[u][:, 0:128], mat("ID"), T.NM[:, 0:128], True, False)
            mm("BO " + key, u, 128, T[u][:, 0:128], mat("BO"), src[:, hs(h)], False, True)
            scan("D0 " + u, "UL%d" % h, 128, T.UL[:, hs(h)], T.D0[:, 0:128], T[u][:, 0:128], -8192.0, Op.min, Op.max)

    SQK = "SQ.0 SQ.1 SQ.2"

    def squares(dst):
        for m in range(2):
            act("UL0 UL1", "%s.%d" % (dst, m), 16, T[dst][:, 16 * m:16 * m + 16], T.UL[:, 15::16], AF.Square, bias=2.0 * KAPPA[m], scale=0.25)
        for m in (2, 3):
            ts("UL0 UL1", "XQ%d" % m, 16, T.XQ[:, 16 * m - 32:16 * m - 16], T.UL[:, 15::16], 0.25, Op.mult, 2.0 * KAPPA[m], Op.add)
        tt("XQ2 XQ3", "%s.2" % dst, 64, T[dst][:, 32:64], T.XQ[:], T.XQ[:], Op.mult)

    def vk():
        for m in range(4):
            ts("VN", "VK%d" % m, 16, T.VK[:, 16 * m:16 * m + 16], lst("VN"), -4.0 * KAPPA[m] ** 2 - 0.25, Op.add)

    def step(t, b):
        if b:
            rowsum(T.Z, "Z0", "Z1")
            squares("SQ")
        for h in range(2):
            src, zk = (T.SD[:, hs(h)], "SD") if b == 0 else (T.Z[:, hs(h)], "Z%d" % h)
            mm("NI " + zk, "pD%d" % h, 128, T["pD%d" % h][:, 0:128], mat("NI"), src, True, False)
        tn = "TN%d" % b
        if b:
            tt(SQK + " VK0 VK1 VK2 VK3", "XI0 XI1 XI2 XI3", 128, T.XI[:], T.SQ[:], T.VK[:], Op.add)
        else:
            for m in range(4):
                tt("SY%d VN" % m, "XI%d" % m, 32, T.XI[:, 16 * m:16 * m + 16], T.SZ[:, 16 * m:16 * m + 16], lst("VN"), Op.add)
        ts("XI0 XI1 XI2 XI3", tn, 64, T.TN[:, 64 * b:64 * b + 64], T.XI[:], W - 1, Op.bitwise_and)
        cp(tn, "OF", 64, T.OF[:], T.TN[:, 64 * b:64 * b + 64])
        for h in range(2):
            boost[0] = AHEAD * (1 - h)
            look = [T.X[:, 0:W].indirect(T.OF[:, 16 * m + 8 * h:16 * m + 8 * h + 8]) for m in range(4)]
            y, d = "Y%d." % h, "pD%d" % h
            ys = [T.Y[:, 256 * m + 128 * h:256 * m + 128 * h + 128] for m in range(4)]
            if h in SFIRST:
                act(XK + " OF", y + "0", looks(128), ys[0], look[0], AF.Copy)
            else:
                cp(XK + " OF", y + "0", looks(128), ys[0], look[0])
            for m in range(1, 4):
                tt("%s OF %s%d" % (XK, y, m - 1), "%s%d" % (y, m), looks(128), ys[m], look[m], ys[m - 1], Op.max)
            mm("ID %s3" % y, d, 128, T[d][:, 0:128], mat("ID"), ys[3], False, True)
            if b < 3:
                act(d, "Z%d" % h, 128, T.Z[:, hs(h)], T[d][:, 0:128], AF.Abs)
            else:
                act(d, "ZF%d.%d" % (t, h), 128, T["ZF%d" % t][:, hs(h)], T[d][:, 0:128], AF.Abs)
        boost[0] = 0.0

    def spread(key, out, src):
        act(src, key, 16, out[:, 0:16], lst(src), AF.Identity, bias=float(D), scale=-float(D))
        for n in (16, 32, 64, 128):
            act(key, key, n, out[:, n:2 * n], out[:, 0:n], AF.Copy)

    def halts(t):
        for h in range(2):
            ts("ZF%d.%d TF" % (t, h), "F%d" % h, 64, T.F[:, hs(h)], T["ZF%d" % t][:, hs(h)], T.TF[:, t:t + 1], Op.is_ge)
        rowsum(T.F, "F0", "F1")
        tt("UL0 UL1 THR", "HA", 32, T.HA[:], T.UL[:, 15::16], lst("THR"), Op.is_ge)
        mm("TG HA", "pC", 16, T.pC[:, 0:16], mat("TG"), T.HA[:], True, False)
        mm("N5 HA", "pC", 16, T.pC[:, 0:16], mat("N5"), T.HA[:], False, False)
        scan("OB HA", "SC1", 16, T.SC[:, 1:17], T.OB[:, 0:16], T.HA[:], 0.0, Op.mult, Op.add)
        mm("BO SC0 SC1", "pC", 16, T.pC[:, 0:16], mat("BO"), T.SC[:, 0:16], False, True)
        ts("pC", "GO", 16, lst("GO"), T.pC[:, 0:16], float(CAP - 512), Op.is_lt)

    def shadows():
        for c in range(16):
            ts("DV VF GO", "EB%d" % c, (L - 16 * c) // 2, T.EB[:, c, 0:L - 16 * c], T.DV[:, 16 * c:L], part("VF", c, c + 1), Op.is_equal, part("GO", c, c + 1), Op.mult)
            if c < 15:
                mm("BK EB%d" % c, "pH", L - 16 - 16 * c, T.pH[:, 272 + 16 * c:512], mat("BK"), T.EB[:, c, 16:L - 16 * c], False, False)
        mm("TK " + " ".join("EB%d" % c for c in range(16)), "pH", 256, T.pH[:, 256:512], mat("TK"), T.EB[:, :, 0:16], False, True)

    def places():
        cp("VN", "OV", 16, T.OV[:], lst("VN"))
        cp("VN", "VF", 16, lst("VF"), lst("VN"))
        cp("OV " + IOK, "DV", looks(256), T.DV[:], T.IO[:].indirect(T.OV[:]))

    def base():
        ts("VC", "S1", 16, lst("S1"), lst("VC"), 4095, Op.bitwise_and)
        tt("S1", "S2", 32, lst("S2"), lst("S1"), lst("S1"), Op.mult)
        ts("S2", "S3", 16, lst("S3"), lst("S2"), 3, Op.arith_shift_right)
        ts("VC", "S4", 16, lst("S4"), lst("VC"), 37.0, Op.mult)
        tt("S3 S4", "BA", 32, lst("BA"), lst("S4"), lst("S3"), Op.add)

    def hits(t, onv):
        mark = 32.0 ** (t + 1 - TS)
        cp("OD OW%d " % t + tabs["HT"], tabs["HT"], puts(256), T.HT[:, 0:8448].indirect(T.OD[:]), T.OW[:, 256 * t:256 * t + 256])
        for k in range(16):
            hb, b0 = "HB%d" % (k % 8), 256 * (k % 8)
            src, key = T.HT[:].indirect(T.OM[:, 16 * k:16 * k + 16]), "%s OM" % tabs["HT"]
            chain[0] = "V" if k in onv else "S"
            if k in onv:
                cp(key, hb, looks(256), T.HB[:, b0:b0 + 256], src)
            else:
                act(key, hb, looks(256), T.HB[:, b0:b0 + 256], src, AF.Copy)
            chain[0] = None
            if k == 0:
                mm("ID NM", "pH", 256, T.pH[:, 0:256], mat("ID"), T.NM[:], True, False)
            mm("ID " + hb, "pH", 256, T.pH[:, 0:256], mat("ID"), T.HB[:, b0:b0 + 256], False, k == 15)
        scan("D0 pH", "HUL", 256, T.HUL[:], T.D0[:], T.pH[:, 0:256], -8192.0, Op.min, Op.max)
        tt("FR recvD%d" % t, "FS", 32, lst("FS"), T["DR%d" % t][:], lst("FR"), Op.add)
        if mark != 1.0:
            ts("FS", "FS", 16, lst("FS"), lst("FS"), mark, Op.mult)
        fr, v = (T.YS[:, 16:32], T.YS[:, 0:16]) if t == TS - 1 else (lst("FR"), lst("VC"))
        tt("VC VN", "S5", 32, lst("S5"), lst("VC"), lst("VN"), Op.subtract)
        tt("HUL FS", "FR", 32, fr, T.HUL[:, 15::16], lst("FS"), Op.is_lt)
        tt("S5 FR", "S6", 32, lst("S6"), lst("S5"), fr, Op.mult)
        tt("S6 VN", "VC", 32, v, lst("S6"), lst("VN"), Op.add)

    def keep():
        ts("FR", "THR", 16, lst("THR"), lst("FR"), 1000.0, Op.mult, 9.0, Op.add)
        base()
        spread("NF", T.NF, "FR")
        ts("NF", "FO", 128, T.FO[:], T.NF[:], -1.0, Op.mult, float(D), Op.add)
        tt("TR NF", "P1", 512, T.P1[:], T.TR[:], T.NF[:], Op.max)

    cp("V0", "VN", 16, lst("VN"), T.V0[:])
    cp("V0", "VC", 16, lst("VC"), T.V0[:])
    rowsum(T.SD, "SD", "SD")
    squares("SZ")
    for m in range(4):
        ts("SZ.%d" % min(m, 2), "SY%d" % m, 16, T.SZ[:, 16 * m:16 * m + 16], T.SZ[:, 16 * m:16 * m + 16], -4.0 * KAPPA[m] ** 2 - 0.25, Op.add)
    base()

    for t in range(TS):
        last = t == TS - 1
        Q = "QA" if t % 2 == 0 else "QB"
        zf = "ZF%d" % t
        vk()
        places()
        for b in range(4):
            step(t, b)
        mm("ID NK", "pH", 256, T.pH[:, 256:512], mat("ID"), T.NK[:], True, False)
        halts(t)
        shadows()
        if not last:
            send(t, "Z", T["ZP%d" % t][:], T[zf][:], zf + ".0 " + zf + ".1")
        scan("D0 pH", "DUL", 256, T.DUL[:], T.D0[:], T.pH[:, 256:512], -8192.0, Op.min, Op.max)
        tt("DUL VF", "L1", 32, lst("L1"), T.DUL[:, 15::16], lst("VF"), Op.max)
        tt("L1 DM", "L2", 32, lst("L2"), lst("L1"), T.DM[:], Op.min)
        lq = "LQ%d" % t
        cp("L2", lq, 16, T[lq][:], lst("L2"))
        send(t, "L", T["RL%d" % t][:], T[lq][:], lq)
        if t < 3:
            wipe("QA" if t == 1 else "QB", 0, 16, lq)
        tn = "TN0 TN1 TN2 TN3"
        spread("NG", T.NG, "GO")
        tt(tn + " NG", "M1", 512, T.M1[:], T.TN[:], T.NG[:], Op.max)
        if t == 0:
            cp("M1", "OM", 256, T.OM[:], T.M1[:])
        else:
            tt("M1 P1", "M2", 512, T.M2[:], T.M1[:], T.P1[:], Op.min)
            cp("M2", "OM", 256, T.OM[:], T.M2[:])
        rl = T["RL%d" % t]
        rk = "recvL%d" % t
        cp("%s CO %s" % (rk, tabs[Q]), tabs[Q], puts(256), T[Q][:, 0:8448].indirect(rl[:]), T.CO[:])
        cp(rk, "LF", 16, lst("LF"), rl[:])
        ts("LF", "IW", 16, lst("IW"), lst("LF"), float(W), Op.is_lt)
        ts("LF", "LD", 16, lst("LD"), lst("LF"), 1.0 / 16384, Op.mult)
        if t == 0:
            cp(tn, "TR", 256, T.TR[:], T.TN[:])
        else:
            tt(tn + " FO", "P2", 512, T.P2[:], T.TN[:], T.FO[:], Op.max)
            tt("P1 P2", "TR", 512, T.TR[:], T.P2[:], T.P1[:], Op.min)
        if last:
            dma("Y", "dy", 32, T.yt[:], T.TR[:], "TR", "yt")

        def turn(k):
            b0, pt, a0 = 512 * k, "pT%d" % (k % 2), 512 * (k % 4)
            for j in range(4):
                op("P", "ID GB%d%s" % (k, "aabb"[j]), pt, 128 * CYC, lambda e, j=j: e.transpose(T[pt][:, POS[j]:POS[j] + 128], T.GB[:, b0 + 128 * j:b0 + 128 * j + 128], mat("ID")))
            for h in range(2):
                a1 = 256 * h
                ts("%s WH%d0 WH%d1" % (pt, h, h), "LA%d" % (k % 4), 128, T.LA[:, a0 + a1:a0 + a1 + 256], T[pt][:, a1:a1 + 256], T.WH[:, h:h + 1], Op.mult)
            ts(pt, "LB%d" % (k % 4), 256, T.LB[:, a0:a0 + 512], T[pt][:, 0:512], -1.0, Op.add, 0.0, Op.max)

        def cells(k):
            for j in range(4):
                a0 = 512 * (k % 4) + 128 * j
                mm("LA%d LB%d" % (k % 4, k % 4), "pC", 128, T.pC[:, 128:256], T.LA[:, a0:a0 + 128], T.LB[:, a0:a0 + 128], k == 0 and j == 0, k == 7 and j == 3)
        for k in range(8):
            key = "%s OM" % tabs[Q]
            if k == 0:
                cp(key, "GB0a", looks(256), T.GB[:, 0:256], T[Q][:].indirect(T.OM[:, 0:16]))
                act(key, "GB0b", looks(256), T.GB[:, 256:512], T[Q][:].indirect(T.OM[:, 16:32]), AF.Copy)
            else:
                act(key, "GB%da GB%db" % (k, k), looks(512), T.GB[:, 512 * k:512 * k + 512], T[Q][:].indirect(T.OM[:, 32 * k:32 * k + 32]), AF.Copy)
        for k in range(8):
            turn(k)
            cells(k)
        tt("pC TH", "MC", 128, T.MC[:], T.pC[:, 128:256], T.TH[:], Op.is_ge)
        tt("MC", "MD", 128, T.MD[:], T.MC[:, 0:64], T.MC[:, 64:128], Op.add)
        tt("MD", "ME", 64, T.ME[:], T.MD[:, 0:32], T.MD[:, 32:64], Op.add)
        tt("ME", "MF", 32, T.MF[:], T.ME[:, 0:16], T.ME[:, 16:32], Op.add)
        do = "DO%d" % t
        tt("MF IW", do, 32, T[do][:], T.MF[:], lst("IW"), Op.is_lt)
        mm("ON " + do, "pC", 16, T.pC[:, 0:16], mat("ON"), T[do][:], True, True)
        send(t, "D", T["DR%d" % t][:], T[do][:], do)
        tt("LD MF", "E1", 32, lst("E1"), T.MF[:], lst("LD"), Op.max)
        tt("E1 DS", "E2", 32, lst("E2"), lst("E1"), lst("DS"), Op.min)
        ts("E2", "OD", 16, T.OD[:], lst("E2"), 16384.0, Op.mult)
        op("V", "pC", "AA", vc(16), lambda e: e.tensor_reduce(T.AA[:], T.pC[:, 0:16], AxisListType.X, Op.add))
        if not last:
            cp("OD recvZ%d" % t, XK, puts(256), T.X[:].indirect(T.OD[:]), T["ZP%d" % t][:])
        ts("BA AA", "S7", 16, lst("S7"), lst("BA"), T.AA[:], Op.add)
        ts("S7", "VN", 16, lst("VN"), lst("S7"), W - 1, Op.bitwise_and)
        if t == 0:
            wipe("QB", 16, 40, "DO0")
        if 0 < t < 3:
            wipe("QA" if t == 1 else "QB", 16, 40, do)
        hits(t, (1, 3, 5, 7, 9, 11, 13, 15) if last else HITS_ON_VECTOR)
        if not last:
            keep()
    dma("Y", "dy", 32, T.ys[:], T.YS[:], "FR VC", "ys")

    N = len(ops)
    preds = [dict() for _ in ops]
    last_w, readers, banks = {}, {}, {}
    ends = {}
    for i, o in enumerate(ops):
        def after(j, wake):
            if j != i:
                preds[i][j] = max(preds[i].get(j, 0.0), wake)
        if o["chain"]:
            if o["chain"] in ends:
                after(ends[o["chain"]], 0.0)
            ends[o["chain"]] = i
        for k in o["r"] + o["w"]:
            if k[0] == "p":
                for q, j in banks.get(k, {}).items():
                    after(j, WAKE if q != o["q"] else 0.0)
        for k in o["r"]:
            if k[0] != "p" and k in last_w:
                after(last_w[k], WAKE)
        for k in o["w"]:
            if k[0] != "p":
                if k in last_w:
                    after(last_w[k], WAKE)
                for j in readers.get(k, []):
                    after(j, WAKE)
        for k in o["r"] + o["w"]:
            if k[0] == "p":
                banks.setdefault(k, {})[o["q"]] = i
        for k in o["r"]:
            if k[0] != "p":
                readers.setdefault(k, []).append(i)
        for k in o["w"]:
            if k[0] != "p":
                last_w[k] = i
                readers[k] = []
    succs = [[] for _ in ops]
    for i in range(N):
        for j, wake in preds[i].items():
            succs[j].append((i, wake))
    prio = [0.0] * N
    for i in range(N - 1, -1, -1):
        best = 0.0
        for j, wake in succs[i]:
            gap = GAP[ops[i]["chain"]] if ops[i]["chain"] and ops[i]["chain"] == ops[j]["chain"] else 0.0
            best = max(best, wake + ops[i]["lat"] + gap + prio[j])
        prio[i] = best + ops[i]["cost"] + ops[i]["first"]
        if STIR:
            prio[i] += STIR * ((i * 7919 + SEED * 104729) * 2654435761 % 4294967296) / 4294967296
    left = [len(preds[i]) for i in range(N)]
    ready = [0.0] * N
    free = {q: 0.0 for q in eng}
    avail = {q: [] for q in eng}
    for i in range(N):
        if left[i] == 0:
            avail[ops[i]["q"]].append(i)
    order = []
    over = [False] * N
    came = [0.0] * N
    line = {q: sorted((i for i in range(N) if ops[i]["q"] == q), key=lambda i: -prio[i]) for q in eng}

    def soonest(i, memo):
        if left[i] == 0:
            return ready[i]
        if i not in memo:
            best = 0.0
            for j, wake in preds[i].items():
                if over[j]:
                    best = max(best, came[j] + ops[j]["lat"] + wake)
                else:
                    best = max(best, max(soonest(j, memo), free[ops[j]["q"]]) + ops[j]["cost"] + ops[j]["lat"] + wake)
            memo[i] = best
        return memo[i]

    order += ORDER
    while len(order) < N:
        pick = None
        for q in "VSPGY":
            if avail[q]:
                t0 = max(free[q], min(ready[i] for i in avail[q]))
                if pick is None or t0 < pick[0]:
                    pick = (t0, q)
        t0, q = pick
        line[q] = [i for i in line[q] if not over[i]]
        memo, i, wait = {}, None, None
        for c in sorted((c for c in avail[q] if ready[c] <= t0), key=lambda c: -prio[c]):
            cost = ops[c]["cost"]
            block = None
            for j in line[q][:8]:
                if j == c or prio[j] < prio[c] + MARGIN * cost:
                    break
                e = soonest(j, memo)
                if t0 < e < t0 + cost - 0.02:
                    block = e if block is None else min(block, e)
            if block is None:
                i = c
                break
            wait = block if wait is None else min(wait, block)
        if i is None:
            free[q] = wait
            continue
        avail[q].remove(i)
        done = t0 + ops[i]["cost"]
        free[q] = came[i] = done
        over[i] = True
        order.append(i)
        for j, wake in succs[i]:
            ready[j] = max(ready[j], done + ops[i]["lat"] + wake)
            left[j] -= 1
            if left[j] == 0:
                avail[ops[j]["q"]].append(j)

    if not ORDER:
        ORDER.extend(order)

    count = {q: 0 for q in eng}
    clock = {q: {} for q in eng}
    wr, rd, bank = {}, {}, {}

    def need(q, tok):
        s, n, known = tok
        if clock[q].get(s, 0) < n:
            eng[q].wait_ge(T.sem[s], n)
            clock[q][s] = n
            for k, m in known.items():
                clock[q][k] = max(clock[q].get(k, 0), m)

    for i in order:
        o = ops[i]
        q, keys = o["q"], o["r"] + o["w"]
        toks = []
        for k in keys:
            if k[0] == "p":
                toks += [tok for q2, tok in bank.get(k, {}).items() if q2 != q]
            elif k in wr:
                toks.append(wr[k])
        for k in o["w"]:
            if k[0] != "p":
                toks += rd.get(k, {}).values()
        best = {}
        for tok in toks:
            if tok[0] not in best or best[tok[0]][1] < tok[1]:
                best[tok[0]] = tok
        for s in sorted(best, key=lambda s: -len(best[s][2])):
            need(q, best[s])
        ins = o["f"](eng[q])
        if o["kind"] == "c":
            ins.then_inc(T.sem["c" + q], 1)
            count[q] += 1
            tok = ("c" + q, count[q], dict(clock[q]))
        elif o["kind"] == "d":
            tok = (o["sem"], o["n"], dict(clock[q]))
        else:
            tok = (o["sem"], o["n"], {})
        for k in keys:
            if k[0] == "p":
                bank.setdefault(k, {})[q] = tok
        for k in o["r"]:
            if k[0] != "p" and o["kind"] != "r":
                rd.setdefault(k, {})[q] = tok
        for k in o["w"]:
            if k[0] != "p":
                wr[k] = tok
                rd[k] = {}
    g.sync.wait_ge(T.sem.dy, 32)
    g.wait_ge(T.sem.loc, sent[0])
    for q in "VSPG":
        g.wait_ge(T.sem["c" + q], count[q])
